import numpy as np
import ml_dtypes


def mxq(x, axis, fmt="e4m3"):
    dtype, down = {"e4m3": (ml_dtypes.float8_e4m3fn, 7), "e5m2": (ml_dtypes.float8_e5m2, 14)}[fmt]
    v = np.moveaxis(np.asarray(x, np.float32).astype(ml_dtypes.bfloat16).astype(np.float64), axis, -1)
    blocks = v.reshape(v.shape[:-1] + (-1, 32))
    amax = np.abs(blocks).max(-1, keepdims=True)
    byte = np.maximum(np.where(amax > 0, np.frexp(amax)[1] - 1 + 127, 0) - down, 1)
    scale = np.exp2(byte - 127.0)
    codes = (blocks / scale).astype(np.float32).astype(dtype).astype(np.float64)
    return np.moveaxis((codes * scale).reshape(v.shape), -1, axis)


WIDE = False


def mx_kscale(k):
    if not WIDE:
        return np.ones(k)
    levels = np.array([10, -10, 5, -5, 0])
    if k % 512:
        return np.exp2(np.random.permutation(np.resize(levels, k // 32))).repeat(32)
    a = np.empty((k // 512, 16))
    for p in range(k // 512):
        a[p, :8] = np.random.permutation(np.resize(levels, 8))
        for g in range(8):
            far = levels[np.abs(levels - a[p, g]) >= 10]
            a[p, g + 8] = far[np.random.randint(len(far))]
    return np.exp2(a.ravel()).repeat(32)


def f64(x):
    return np.asarray(x).astype(np.float64)


def striped(idx):
    return np.tile(np.asarray(idx).reshape(-1, 16).T, (8, 1)).astype(np.uint16)


def unstriped(offs):
    return offs[:16].T.reshape(-1).astype(np.int64)


E2M1 = np.array([0.0, 0.5, 1.0, 1.5, 2.0, 3.0, 4.0, 6.0, -0.0, -0.5, -1.0, -1.5, -2.0, -3.0, -4.0, -6.0])


def pack_weight(w, fmt):
    k, n = w.shape
    w = f64(np.asarray(w, np.float32).astype(ml_dtypes.bfloat16)).reshape(k // 32, 32, n)
    amax = np.abs(w).max(1)
    if fmt == "e4m3":
        byte = np.frexp(amax)[1] - 1 + 127 - 7
    else:
        mant, ex = np.frexp(amax / 6.0)
        byte = np.where(mant > 0.5, ex, ex - 1) + 127
    byte = np.clip(np.where(amax > 0, byte, 1), 1, 254)
    scaled = (w * np.exp2(127.0 - byte)[:, None, :]).reshape(k, n).astype(np.float32)
    by_word = np.ascontiguousarray(scaled.reshape(k // 512, 128, 4, n).transpose(0, 1, 3, 2))
    if fmt == "e4m3":
        words = by_word.astype(ml_dtypes.float8_e4m3fn).view(np.uint8)
    else:
        c = by_word.astype(ml_dtypes.float4_e2m1fn).view(np.uint8) & 0xF
        words = (c[..., 0::2] | (c[..., 1::2] << 4)).reshape(k // 512, 128, 2 * n)
    return np.ascontiguousarray(words), np.ascontiguousarray(byte.astype(np.uint8).reshape(k // 512, 16, n))


def unpack_weight(words, scales, fmt):
    g, _, n = scales.shape
    words = np.ascontiguousarray(words).reshape(g, 128, n, -1)
    if fmt == "e4m3":
        vals = words.view(ml_dtypes.float8_e4m3fn).astype(np.float64)
    else:
        nib = np.empty((g, 128, n, 4), np.uint8)
        nib[..., 0::2] = words & 0xF
        nib[..., 1::2] = words >> 4
        vals = E2M1[nib]
    vals = vals * np.repeat(np.exp2(scales.astype(np.float64) - 127.0), 8, axis=1)[..., None]
    return vals.transpose(0, 1, 3, 2).reshape(g * 512, n)


B, N, T, D, DV, NQ = 1, 512, 2048, 512, 256, 256


def setup_inputs():
    n = np.random.standard_normal
    idx = np.random.permutation(T)[:B * N]
    s = mx_kscale(D)[:, None]
    u = np.ones(T)
    u[idx] = mx_kscale(B * N)
    r = np.random.uniform(0.5, 2.0, T)
    qidx = np.random.permutation(T)[:B * NQ]
    k = n((D, T)) / s
    v = n((DV, T)) / (u * r)
    kp = pack_weight(k, "e4m3")
    return {
        "xq": (n((D, T)) * s * (0.80 / np.sqrt(D))).astype(np.float32),
        "k_words": kp[0],
        "k_scales": kp[1],
        "vT": v.astype(np.float32),
        "vs": np.tile(u * r, (128, 1)).astype(np.float32),
        "offs": striped(idx),
        "qoffs": striped(qidx),
    }


def reference(xq, k_words, k_scales, vT, vs, offs, qoffs):
    idx = unstriped(offs)
    k = unpack_weight(k_words, k_scales, "e4m3")
    v = f64(vT)
    pick = lambda x: x[:, idx].reshape(x.shape[0], B, N).transpose(1, 0, 2)
    q = f64(xq)[:, unstriped(qoffs)].reshape(D, B, NQ).transpose(1, 0, 2)
    score = mxq(q, 1, "e4m3").transpose(0, 2, 1) @ pick(k)
    m = score.max(-1, keepdims=True)
    p = np.exp(score - m)
    total = p.sum(-1, keepdims=True)
    w = p * pick(f64(vs))[:, :1, :]
    y = mxq(w, 2, "e4m3") @ mxq(pick(v).transpose(0, 2, 1), 1, "e4m3")
    y = y / total
    out = np.zeros((DV, T))
    out[:, unstriped(qoffs)] = y.transpose(2, 0, 1).reshape(-1, B * NQ)
    return out

@@ -1,0 +1,174 @@
+from contextlib import ExitStack
+
+import concourse.mybir as mybir
+from concourse.masks import make_identity
+
+F32 = mybir.dt.float32
+BF16 = mybir.dt.bfloat16
+I32 = mybir.dt.int32
+U32 = mybir.dt.uint32
+U16 = mybir.dt.uint16
+U8 = mybir.dt.uint8
+FP8X4 = mybir.dt.float8_e4m3fn_x4
+ACT = mybir.ActivationFunctionType
+ALU = mybir.AluOpType
+AX = mybir.AxisListType
+
+P = 128
+PACK = 4
+T, D, DV, N, NQ = 2048, 512, 256, 512, 256
+QB = NQ // P
+EB = DV // P
+
+FLOPS = 2 * NQ * N * (D + DV)
+BYTES = 4 * D * T + D * T + (D // 32) * T + 4 * DV * T + 4 * T + 2 * P * (N + NQ) // 16 + 4 * DV * T
+
+
+def tile_attend_router_kernel(tc, xq, k_words, k_scales, vT, vs, offs, qoffs, out):
+    nc = tc.nc
+    with ExitStack() as ctx:
+        sb = ctx.enter_context(tc.tile_pool(name="sb", bufs=1))
+        ps = ctx.enter_context(tc.psum_pool(name="ps", bufs=1))
+
+        slot_list = sb.tile([P, N // 16], U16, name="slot_list")
+        query_list = sb.tile([P, NQ // 16], U16, name="query_list")
+        xq_pool = [sb.tile([P, T], F32, name=f"xq_pool{t}") for t in range(PACK)]
+        kw_pool = sb.tile([P, T], I32, name="kw_pool")
+        ks_pool = sb.tile([P, T], U8, name="ks_pool")
+        vs_pool = sb.tile([P, T], F32, name="vs_pool")
+        v_pool = [sb.tile([P, T], F32, name=f"v_pool{h}") for h in range(EB)]
+        result = [sb.tile([P, T], F32, name=f"result{h}") for h in range(EB)]
+
+        nc.vector.memset(ks_pool[:].bitcast(I32), 0)
+        nc.vector.memset(vs_pool[:], 0.0)
+
+        xq_planes = xq.rearrange("(p t) n -> p t n", t=PACK)
+        ks_rows = k_scales[0].bitcast(I32)
+        nc.sync.dma_start(xq_pool[0][:], xq_planes[:, 0, :])
+        nc.sync.dma_start(query_list[:], qoffs)
+        nc.sync.dma_start(xq_pool[1][:], xq_planes[:, 1, :])
+        nc.sync.dma_start(slot_list[:], offs)
+        for g in range(4):
+            nc.sync.dma_start(ks_pool[32 * g : 32 * g + 4, :].bitcast(I32), ks_rows[4 * g : 4 * g + 4, :])
+        nc.sync.dma_start(vs_pool[0:1, :], vs[0:1, :])
+        nc.sync.dma_start(xq_pool[2][:], xq_planes[:, 2, :])
+        nc.sync.dma_start(xq_pool[3][:], xq_planes[:, 3, :])
+        nc.sync.dma_start(kw_pool[:], k_words[0].rearrange("p n t -> p (n t)").bitcast(I32))
+        for h in range(EB):
+            nc.sync.dma_start(v_pool[h][:], vT[h * P : (h + 1) * P, :])
+
+        ident = sb.tile([P, P], F32, name="ident")
+        make_identity(nc, ident[:])
+        warm = sb.tile([P, 1], F32, name="warm")
+        nc.scalar.activation(warm[:], ident[:, 0:1], ACT.Exp)
+        for h in range(EB):
+            nc.vector.memset(result[h][:], 0.0)
+
+        q_bf = sb.tile([P, NQ, PACK], BF16, name="q_bf", align_bytes=64)
+
+        def gather_queries(t):
+            nc.vector.tensor_copy(q_bf[:, :, t], xq_pool[t][:].indirect(query_list[:]))
+
+        gather_queries(0)
+        gather_queries(1)
+
+        k_codes = sb.tile([P, N], U32, name="k_codes", align_bytes=64)
+        k_bytes = sb.tile([P, N], U8, name="k_bytes", align_bytes=64)
+        vs_row = sb.tile([P, N], F32, name="vs_row")
+        nc.vector.tensor_copy(k_bytes[:], ks_pool[:].indirect(slot_list[:]))
+        nc.vector.tensor_copy(vs_row[:], vs_pool[:].indirect(slot_list[:]))
+
+        vs_ps = ps.tile([P, PACK, P], F32, name="vs_ps", tag="aux")
+        for t in range(PACK):
+            nc.tensor.transpose(vs_ps[:, t, :], vs_row[:, t : N : PACK], ident[:])
+        vs_col = sb.tile([P, PACK], F32, name="vs_col")
+        nc.scalar.copy(vs_col[:], vs_ps[:, :, 0])
+
+        gather_queries(2)
+        gather_queries(3)
+
+        q_codes = sb.tile([P, NQ], U32, name="q_codes", align_bytes=64)
+        q_bytes = sb.tile([P, NQ], U8, name="q_bytes", align_bytes=64)
+        q_flat = q_bf[:].rearrange("p q t -> p (q t)")
+        scores = []
+        for b in range(QB):
+            cols = slice(b * P, (b + 1) * P)
+            nc.vector.quantize_mx(out=q_codes[:, cols].bitcast(FP8X4), scales=q_bytes[:, cols],
+                                  in_=q_flat[:, b * P * PACK : (b + 1) * P * PACK])
+            scores.append(ps.tile([P, N], F32, name=f"score{b}", tag=f"acc{b}"))
+        half = N // 2
+        for j in range(2):
+            slots = slice(j * half, (j + 1) * half)
+            nc.vector.tensor_copy(k_codes[:, slots],
+                                  kw_pool[:].bitcast(U32).indirect(slot_list[:, j * half // 16 : (j + 1) * half // 16]))
+            for b in range(QB):
+                cols = slice(b * P, (b + 1) * P)
+                nc.tensor.matmul_mx(out=scores[b][:, slots], lhsT=q_codes[:, cols].bitcast(FP8X4), lhsT_scale=q_bytes[:, cols],
+                                    rhs=k_codes[:, slots].bitcast(FP8X4), rhs_scale=k_bytes[:, slots], start=True, stop=True)
+
+        row_sum = sb.tile([P, QB], F32, name="row_sum")
+        p_turned = []
+        for b in range(QB):
+            neg_max = sb.tile([P, 1], F32, name=f"neg_max{b}")
+            nc.vector.tensor_reduce(neg_max[:], scores[b][:], AX.X, ALU.max, negate=True)
+            p = sb.tile([P, PACK, P], F32, name=f"p{b}")
+            nc.scalar.activation(p[:], scores[b][:].rearrange("q (s t) -> q t s", t=PACK), ACT.Exp,
+                                 bias=neg_max[:], accum_out=row_sum[:, b : b + 1])
+            pt = ps.tile([P, PACK, P], F32, name=f"pt{b}")
+            for t in range(PACK):
+                nc.tensor.transpose(pt[:, t, :], p[:, t, :], ident[:])
+            p_turned.append(pt)
+
+        v_codes = [sb.tile([P, P], U32, name=f"v_codes{h}", align_bytes=64) for h in range(EB)]
+        v_bytes = [sb.tile([P, P], U8, name=f"v_bytes{h}", align_bytes=64) for h in range(EB)]
+        v_bf = [sb.tile([P, P * PACK], BF16, name=f"v_bf{h}", align_bytes=64) for h in range(EB)]
+
+        def turn_values(h):
+            picked = sb.tile([P, 2, P, 2], BF16, name=f"v_picked{h}")
+            nc.vector.tensor_copy(picked[:].rearrange("p u s e -> p s u e"), v_pool[h][:].indirect(slot_list[:]))
+            pairs = picked[:].rearrange("p u s e -> p (u s e)").bitcast(F32)
+            vt = ps.tile([P, 2, P], F32, name=f"vt{h}")
+            for u in range(2):
+                nc.tensor.transpose(vt[:, u, :], pairs[:, u * P : (u + 1) * P], ident[:])
+            nc.scalar.copy(v_bf[h][:].bitcast(F32).rearrange("s (r u) -> s r u", u=2), vt[:].rearrange("s u r -> s r u"))
+
+        def quantize_values(h):
+            nc.vector.quantize_mx(out=v_codes[h][:].bitcast(FP8X4), scales=v_bytes[h][:], in_=v_bf[h][:])
+
+        turn_values(0)
+
+        w_bf = sb.tile([P, NQ, PACK], BF16, name="w_bf", align_bytes=64)
+        w_codes = sb.tile([P, NQ], U32, name="w_codes", align_bytes=64)
+        w_bytes = sb.tile([P, NQ], U8, name="w_bytes", align_bytes=64)
+        w_flat = w_bf[:].rearrange("s q t -> s (q t)")
+        vs_wide = vs_col[:].unsqueeze(1).to_broadcast([P, P, PACK])
+        for b in range(QB):
+            nc.vector.tensor_tensor(w_bf[:, b * P : (b + 1) * P, :], p_turned[b][:].rearrange("s t q -> s q t"),
+                                    vs_wide, ALU.mult)
+        quantize_values(0)
+        for b in range(QB):
+            cols = slice(b * P, (b + 1) * P)
+            nc.vector.quantize_mx(out=w_codes[:, cols].bitcast(FP8X4), scales=w_bytes[:, cols],
+                                  in_=w_flat[:, b * P * PACK : (b + 1) * P * PACK])
+
+        inv_sum = sb.tile([P, QB], F32, name="inv_sum")
+        nc.vector.reciprocal(inv_sum[:], row_sum[:])
+        inv_ps = ps.tile([P, QB, P], F32, name="inv_ps", tag="aux")
+        for b in range(QB):
+            nc.tensor.transpose(inv_ps[:, b, :], inv_sum[:, b : b + 1].to_broadcast([P, P]), ident[:])
+        inv_wide = sb.tile([P, NQ], F32, name="inv_wide")
+        nc.scalar.copy(inv_wide[:], inv_ps[:].rearrange("p b q -> p (b q)"))
+
+        def finish(h):
+            y = ps.tile([P, NQ], F32, name=f"y{h}", tag=f"acc{h}")
+            nc.tensor.matmul_mx(out=y[:], lhsT=v_codes[h][:].bitcast(FP8X4), lhsT_scale=v_bytes[h][:],
+                                rhs=w_codes[:].bitcast(FP8X4), rhs_scale=w_bytes[:], start=True, stop=True)
+            y_sb = sb.tile([P, NQ], F32, name=f"y_sb{h}")
+            nc.scalar.copy(y_sb[:], y[:])
+            nc.vector.tensor_tensor(result[h][:].indirect(query_list[:]), y_sb[:], inv_wide[:], ALU.mult)
+            nc.sync.dma_start(out[h * P : (h + 1) * P, :], result[h][:])
+
+        turn_values(1)
+        finish(0)
+        quantize_values(1)
+        finish(1)

@@ -19,6 +19,7 @@ PACK = 4
 T, D, DV, N, NQ = 2048, 512, 256, 512, 256
 QB = NQ // P
 EB = DV // P
+VS_ROW = 16
 
 FLOPS = 2 * NQ * N * (D + DV)
 BYTES = 4 * D * T + D * T + (D // 32) * T + 4 * DV * T + 4 * T + 2 * P * (N + NQ) // 16 + 4 * DV * T
@@ -48,9 +49,9 @@ def tile_attend_router_kernel(tc, xq, k_words, k_scales, vT, vs, offs, qoffs, ou
         nc.sync.dma_start(query_list[:], qoffs)
         nc.sync.dma_start(xq_pool[1][:], xq_planes[:, 1, :])
         nc.sync.dma_start(slot_list[:], offs)
-        for g in range(4):
-            nc.sync.dma_start(ks_pool[32 * g : 32 * g + 4, :].bitcast(I32), ks_rows[4 * g : 4 * g + 4, :])
-        nc.sync.dma_start(vs_pool[0:1, :], vs[0:1, :])
+        for r in range(4):
+            nc.sync.dma_start(ks_pool[r:P:32, :].bitcast(I32), ks_rows[r:16:4, :])
+        nc.sync.dma_start(vs_pool[VS_ROW : VS_ROW + 1, :], vs[0:1, :])
         nc.sync.dma_start(xq_pool[2][:], xq_planes[:, 2, :])
         nc.sync.dma_start(xq_pool[3][:], xq_planes[:, 3, :])
         nc.sync.dma_start(kw_pool[:], k_words[0].rearrange("p n t -> p (n t)").bitcast(I32))
@@ -62,7 +63,7 @@ def tile_attend_router_kernel(tc, xq, k_words, k_scales, vT, vs, offs, qoffs, ou
         warm = sb.tile([P, 1], F32, name="warm")
         nc.scalar.activation(warm[:], ident[:, 0:1], ACT.Exp)
         for h in range(EB):
-            nc.vector.memset(result[h][:], 0.0)
+            nc.gpsimd.memset(result[h][:], 0.0)
 
         q_bf = sb.tile([P, NQ, PACK], BF16, name="q_bf", align_bytes=64)
 
@@ -82,7 +83,7 @@ def tile_attend_router_kernel(tc, xq, k_words, k_scales, vT, vs, offs, qoffs, ou
         for t in range(PACK):
             nc.tensor.transpose(vs_ps[:, t, :], vs_row[:, t : N : PACK], ident[:])
         vs_col = sb.tile([P, PACK], F32, name="vs_col")
-        nc.scalar.copy(vs_col[:], vs_ps[:, :, 0])
+        nc.scalar.copy(vs_col[:], vs_ps[:, :, VS_ROW])
 
         gather_queries(2)
         gather_queries(3)
@@ -145,14 +146,14 @@ def tile_attend_router_kernel(tc, xq, k_words, k_scales, vT, vs, offs, qoffs, ou
         for b in range(QB):
             nc.vector.tensor_tensor(w_bf[:, b * P : (b + 1) * P, :], p_turned[b][:].rearrange("s t q -> s q t"),
                                     vs_wide, ALU.mult)
+        inv_sum = sb.tile([P, QB], F32, name="inv_sum")
+        nc.vector.reciprocal(inv_sum[:], row_sum[:])
         quantize_values(0)
         for b in range(QB):
             cols = slice(b * P, (b + 1) * P)
             nc.vector.quantize_mx(out=w_codes[:, cols].bitcast(FP8X4), scales=w_bytes[:, cols],
                                   in_=w_flat[:, b * P * PACK : (b + 1) * P * PACK])
 
-        inv_sum = sb.tile([P, QB], F32, name="inv_sum")
-        nc.vector.reciprocal(inv_sum[:], row_sum[:])
         inv_ps = ps.tile([P, QB, P], F32, name="inv_ps", tag="aux")
         for b in range(QB):
             nc.tensor.transpose(inv_ps[:, b, :], inv_sum[:, b : b + 1].to_broadcast([P, P]), ident[:])

@@ -109,15 +109,19 @@ def tile_attend_router_kernel(tc, xq, k_words, k_scales, vT, vs, offs, qoffs, ou
 
         row_sum = sb.tile([P, QB], F32, name="row_sum")
         p_turned = []
+        probs = []
         for b in range(QB):
             neg_max = sb.tile([P, 1], F32, name=f"neg_max{b}")
             nc.vector.tensor_reduce(neg_max[:], scores[b][:], AX.X, ALU.max, negate=True)
             p = sb.tile([P, PACK, P], F32, name=f"p{b}")
             nc.scalar.activation(p[:], scores[b][:].rearrange("q (s t) -> q t s", t=PACK), ACT.Exp,
                                  bias=neg_max[:], accum_out=row_sum[:, b : b + 1])
+            probs.append(p)
+
+        def turn_weights(b):
             pt = ps.tile([P, PACK, P], F32, name=f"pt{b}")
             for t in range(PACK):
-                nc.tensor.transpose(pt[:, t, :], p[:, t, :], ident[:])
+                nc.tensor.transpose(pt[:, t, :], probs[b][:, t, :], ident[:])
             p_turned.append(pt)
 
         v_codes = [sb.tile([P, P], U32, name=f"v_codes{h}", align_bytes=64) for h in range(EB)]
@@ -136,6 +140,8 @@ def tile_attend_router_kernel(tc, xq, k_words, k_scales, vT, vs, offs, qoffs, ou
         def quantize_values(h):
             nc.vector.quantize_mx(out=v_codes[h][:].bitcast(FP8X4), scales=v_bytes[h][:], in_=v_bf[h][:])
 
+        turn_weights(0)
+        turn_weights(1)
         turn_values(0)
 
         w_bf = sb.tile([P, NQ, PACK], BF16, name="w_bf", align_bytes=64)
@@ -165,8 +171,12 @@ def tile_attend_router_kernel(tc, xq, k_words, k_scales, vT, vs, offs, qoffs, ou
             nc.tensor.matmul_mx(out=y[:], lhsT=v_codes[h][:].bitcast(FP8X4), lhsT_scale=v_bytes[h][:],
                                 rhs=w_codes[:].bitcast(FP8X4), rhs_scale=w_bytes[:], start=True, stop=True)
             y_sb = sb.tile([P, NQ], F32, name=f"y_sb{h}")
-            nc.scalar.copy(y_sb[:], y[:])
-            nc.vector.tensor_tensor(result[h][:].indirect(query_list[:]), y_sb[:], inv_wide[:], ALU.mult)
+            if h == 0:
+                nc.scalar.copy(y_sb[:], y[:])
+                nc.vector.tensor_tensor(result[h][:].indirect(query_list[:]), y_sb[:], inv_wide[:], ALU.mult)
+            else:
+                nc.vector.tensor_tensor(y_sb[:], y[:], inv_wide[:], ALU.mult)
+                nc.vector.tensor_copy(result[h][:].indirect(query_list[:]), y_sb[:])
             nc.sync.dma_start(out[h * P : (h + 1) * P, :], result[h][:])
 
         turn_values(1)

@@ -29,6 +29,7 @@ def tile_attend_router_kernel(tc, xq, k_words, k_scales, vT, vs, offs, qoffs, ou
     nc = tc.nc
     with ExitStack() as ctx:
         sb = ctx.enter_context(tc.tile_pool(name="sb", bufs=1))
+        late = ctx.enter_context(tc.tile_pool(name="late", bufs=1))
         ps = ctx.enter_context(tc.psum_pool(name="ps", bufs=1))
 
         slot_list = sb.tile([P, N // 16], U16, name="slot_list")
@@ -37,7 +38,7 @@ def tile_attend_router_kernel(tc, xq, k_words, k_scales, vT, vs, offs, qoffs, ou
         kw_pool = sb.tile([P, T], I32, name="kw_pool")
         ks_pool = sb.tile([P, T], U8, name="ks_pool")
         vs_pool = sb.tile([P, T], F32, name="vs_pool")
-        v_pool = [sb.tile([P, T], F32, name=f"v_pool{h}") for h in range(EB)]
+        v_pool = [sb.tile([P, T], F32, name="v_pool0"), late.tile([P, T], F32, name="v_pool1", align_bytes=64, offset=0)]
         result = [sb.tile([P, T], F32, name=f"result{h}") for h in range(EB)]
 
         nc.vector.memset(ks_pool[:].bitcast(I32), 0)
@@ -96,26 +97,33 @@ def tile_attend_router_kernel(tc, xq, k_words, k_scales, vT, vs, offs, qoffs, ou
             cols = slice(b * P, (b + 1) * P)
             nc.vector.quantize_mx(out=q_codes[:, cols].bitcast(FP8X4), scales=q_bytes[:, cols],
                                   in_=q_flat[:, b * P * PACK : (b + 1) * P * PACK])
-            scores.append(ps.tile([P, N], F32, name=f"score{b}", tag=f"acc{b}"))
         half = N // 2
+        for b in range(QB):
+            scores.append([ps.tile([P, half], F32, name=f"score{b}_{j}", tag=f"acc{b}_{j}") for j in range(2)])
         for j in range(2):
             slots = slice(j * half, (j + 1) * half)
             nc.vector.tensor_copy(k_codes[:, slots],
                                   kw_pool[:].bitcast(U32).indirect(slot_list[:, j * half // 16 : (j + 1) * half // 16]))
             for b in range(QB):
                 cols = slice(b * P, (b + 1) * P)
-                nc.tensor.matmul_mx(out=scores[b][:, slots], lhsT=q_codes[:, cols].bitcast(FP8X4), lhsT_scale=q_bytes[:, cols],
+                nc.tensor.matmul_mx(out=scores[b][j][:], lhsT=q_codes[:, cols].bitcast(FP8X4), lhsT_scale=q_bytes[:, cols],
                                     rhs=k_codes[:, slots].bitcast(FP8X4), rhs_scale=k_bytes[:, slots], start=True, stop=True)
 
         row_sum = sb.tile([P, QB], F32, name="row_sum")
         p_turned = []
         probs = []
+        neg_score = [sb.tile([P, PACK, P], F32, name=f"neg_score{b}") for b in range(QB)]
+        neg_max = [[sb.tile([P, 1], F32, name=f"neg_max{b}_{j}") for j in range(2)] for b in range(QB)]
+        for j in range(2):
+            for b in range(QB):
+                nc.vector.tensor_scalar(neg_score[b][:, :, j * P // 2 : (j + 1) * P // 2],
+                                        scores[b][j][:].rearrange("q (s t) -> q t s", t=PACK),
+                                        -1.0, neg_max[b][0][:] if j else None, ALU.mult, ALU.min,
+                                        accum_out=neg_max[b][j][:])
         for b in range(QB):
-            neg_max = sb.tile([P, 1], F32, name=f"neg_max{b}")
-            nc.vector.tensor_reduce(neg_max[:], scores[b][:], AX.X, ALU.max, negate=True)
             p = sb.tile([P, PACK, P], F32, name=f"p{b}")
-            nc.scalar.activation(p[:], scores[b][:].rearrange("q (s t) -> q t s", t=PACK), ACT.Exp,
-                                 bias=neg_max[:], accum_out=row_sum[:, b : b + 1])
+            nc.scalar.activation(p[:], neg_score[b][:], ACT.Exp, scale=-1.0,
+                                 bias=neg_max[b][1][:], accum_out=row_sum[:, b : b + 1])
             probs.append(p)
 
         def turn_weights(b):
@@ -124,7 +132,8 @@ def tile_attend_router_kernel(tc, xq, k_words, k_scales, vT, vs, offs, qoffs, ou
                 nc.tensor.transpose(pt[:, t, :], probs[b][:, t, :], ident[:])
             p_turned.append(pt)
 
-        v_codes = [sb.tile([P, P], U32, name=f"v_codes{h}", align_bytes=64) for h in range(EB)]
+        v_codes = [late.tile([P, P], U32, name="v_codes0", align_bytes=64, offset=0),
+                   sb.tile([P, P], U32, name="v_codes1", align_bytes=64)]
         v_bytes = [sb.tile([P, P], U8, name=f"v_bytes{h}", align_bytes=64) for h in range(EB)]
         v_bf = [sb.tile([P, P * PACK], BF16, name=f"v_bf{h}", align_bytes=64) for h in range(EB)]
 
@@ -132,7 +141,7 @@ def tile_attend_router_kernel(tc, xq, k_words, k_scales, vT, vs, offs, qoffs, ou
             picked = sb.tile([P, 2, P, 2], BF16, name=f"v_picked{h}")
             nc.vector.tensor_copy(picked[:].rearrange("p u s e -> p s u e"), v_pool[h][:].indirect(slot_list[:]))
             pairs = picked[:].rearrange("p u s e -> p (u s e)").bitcast(F32)
-            vt = ps.tile([P, 2, P], F32, name=f"vt{h}")
+            vt = ps.tile([P, 2, P], F32, name=f"vt{h}", tag="vt")
             for u in range(2):
                 nc.tensor.transpose(vt[:, u, :], pairs[:, u * P : (u + 1) * P], ident[:])
             nc.scalar.copy(v_bf[h][:].bitcast(F32).rearrange("s (r u) -> s r u", u=2), vt[:].rearrange("s u r -> s r u"))
@@ -140,46 +149,53 @@ def tile_attend_router_kernel(tc, xq, k_words, k_scales, vT, vs, offs, qoffs, ou
         def quantize_values(h):
             nc.vector.quantize_mx(out=v_codes[h][:].bitcast(FP8X4), scales=v_bytes[h][:], in_=v_bf[h][:])
 
-        turn_weights(0)
-        turn_weights(1)
-        turn_values(0)
-
-        w_bf = sb.tile([P, NQ, PACK], BF16, name="w_bf", align_bytes=64)
-        w_codes = sb.tile([P, NQ], U32, name="w_codes", align_bytes=64)
+        w_bf = [sb.tile([P, P, PACK], BF16, name="w_bf0", align_bytes=64),
+                late.tile([P, P, PACK], BF16, name="w_bf1", align_bytes=64, offset=512)]
+        w_codes = late.tile([P, NQ], U32, name="w_codes", align_bytes=64, offset=1536)
         w_bytes = sb.tile([P, NQ], U8, name="w_bytes", align_bytes=64)
-        w_flat = w_bf[:].rearrange("s q t -> s (q t)")
         vs_wide = vs_col[:].unsqueeze(1).to_broadcast([P, P, PACK])
-        for b in range(QB):
-            nc.vector.tensor_tensor(w_bf[:, b * P : (b + 1) * P, :], p_turned[b][:].rearrange("s t q -> s q t"),
-                                    vs_wide, ALU.mult)
-        inv_sum = sb.tile([P, QB], F32, name="inv_sum")
-        nc.vector.reciprocal(inv_sum[:], row_sum[:])
-        quantize_values(0)
-        for b in range(QB):
+
+        def weigh(b):
+            nc.vector.tensor_tensor(w_bf[b][:], p_turned[b][:].rearrange("s t q -> s q t"), vs_wide, ALU.mult)
+
+        def quantize_weights(b):
             cols = slice(b * P, (b + 1) * P)
             nc.vector.quantize_mx(out=w_codes[:, cols].bitcast(FP8X4), scales=w_bytes[:, cols],
-                                  in_=w_flat[:, b * P * PACK : (b + 1) * P * PACK])
+                                  in_=w_bf[b][:].rearrange("s q t -> s (q t)"))
 
+        inv_sum = late.tile([P, QB], F32, name="inv_sum", align_bytes=64, offset=3584)
+        inv_wide = late.tile([P, NQ], F32, name="inv_wide", align_bytes=64, offset=2560)
+        y_sb = [sb.tile([P, NQ], F32, name=f"y_sb{h}") for h in range(EB)]
+
+        def product(h, cols, tag):
+            y = ps.tile([P, cols.stop - cols.start], F32, name=f"y_{tag}", tag=tag)
+            nc.tensor.matmul_mx(out=y[:], lhsT=v_codes[h][:].bitcast(FP8X4), lhsT_scale=v_bytes[h][:],
+                                rhs=w_codes[:, cols].bitcast(FP8X4), rhs_scale=w_bytes[:, cols], start=True, stop=True)
+            nc.scalar.copy(y_sb[h][:, cols], y[:])
+
+        def finish(h):
+            nc.vector.tensor_tensor(result[h][:].indirect(query_list[:]), y_sb[h][:], inv_wide[:], ALU.mult)
+            nc.sync.dma_start(out[h * P : (h + 1) * P, :], result[h][:])
+
+        turn_weights(0)
+        w_planes = sb.tile([P, PACK, P], BF16, name="w_planes")
+        for t in range(PACK):
+            nc.scalar.activation(w_planes[:, t, :], p_turned[0][:, t, :], ACT.Copy, scale=vs_col[:, t : t + 1])
+        turn_values(0)
+        nc.scalar.copy(w_bf[0][:].rearrange("s (c i) t -> s c t i", i=4), w_planes[:].rearrange("s t (c i) -> s c t i", i=4))
+        turn_weights(1)
+        turn_values(1)
+        weigh(1)
+        nc.vector.reciprocal(inv_sum[:], row_sum[:])
         inv_ps = ps.tile([P, QB, P], F32, name="inv_ps", tag="aux")
         for b in range(QB):
             nc.tensor.transpose(inv_ps[:, b, :], inv_sum[:, b : b + 1].to_broadcast([P, P]), ident[:])
-        inv_wide = sb.tile([P, NQ], F32, name="inv_wide")
-        nc.scalar.copy(inv_wide[:], inv_ps[:].rearrange("p b q -> p (b q)"))
-
-        def finish(h):
-            y = ps.tile([P, NQ], F32, name=f"y{h}", tag=f"acc{h}")
-            nc.tensor.matmul_mx(out=y[:], lhsT=v_codes[h][:].bitcast(FP8X4), lhsT_scale=v_bytes[h][:],
-                                rhs=w_codes[:].bitcast(FP8X4), rhs_scale=w_bytes[:], start=True, stop=True)
-            y_sb = sb.tile([P, NQ], F32, name=f"y_sb{h}")
-            if h == 0:
-                nc.scalar.copy(y_sb[:], y[:])
-                nc.vector.tensor_tensor(result[h][:].indirect(query_list[:]), y_sb[:], inv_wide[:], ALU.mult)
-            else:
-                nc.vector.tensor_tensor(y_sb[:], y[:], inv_wide[:], ALU.mult)
-                nc.vector.tensor_copy(result[h][:].indirect(query_list[:]), y_sb[:])
-            nc.sync.dma_start(out[h * P : (h + 1) * P, :], result[h][:])
-
-        turn_values(1)
-        finish(0)
+        quantize_values(0)
+        for b in reversed(range(QB)):
+            quantize_weights(b)
+            product(0, slice(b * P, (b + 1) * P), f"acc0_{b}")
         quantize_values(1)
+        nc.vector.tensor_copy(inv_wide[:], inv_ps[:].rearrange("p b q -> p (b q)"))
+        product(1, slice(0, NQ), "acc1_0")
+        finish(0)
         finish(1)

@@ -19,7 +19,8 @@ PACK = 4
 T, D, DV, N, NQ = 2048, 512, 256, 512, 256
 QB = NQ // P
 EB = DV // P
-VS_ROW = 16
+VS_ROW = 4
+KS_STEP = 8
 
 FLOPS = 2 * NQ * N * (D + DV)
 BYTES = 4 * D * T + D * T + (D // 32) * T + 4 * DV * T + 4 * T + 2 * P * (N + NQ) // 16 + 4 * DV * T
@@ -34,30 +35,26 @@ def tile_attend_router_kernel(tc, xq, k_words, k_scales, vT, vs, offs, qoffs, ou
 
         slot_list = sb.tile([P, N // 16], U16, name="slot_list")
         query_list = sb.tile([P, NQ // 16], U16, name="query_list")
-        xq_pool = [sb.tile([P, T], F32, name=f"xq_pool{t}") for t in range(PACK)]
-        kw_pool = sb.tile([P, T], I32, name="kw_pool")
-        ks_pool = sb.tile([P, T], U8, name="ks_pool")
+        xq_pool = [sb.tile([P, T], F32, name="xq_pool0", tag="first"),
+                   late.tile([P, T], F32, name="xq_pool1", align_bytes=64, offset=0),
+                   sb.tile([P, T], F32, name="xq_pool2"), sb.tile([P, T], F32, name="xq_pool3")]
+        ks_pool = sb.tile([P, T], U8, name="ks_pool", tag="keys")
         vs_pool = sb.tile([P, T], F32, name="vs_pool")
-        v_pool = [sb.tile([P, T], F32, name="v_pool0"), late.tile([P, T], F32, name="v_pool1", align_bytes=64, offset=0)]
         result = [sb.tile([P, T], F32, name=f"result{h}") for h in range(EB)]
 
-        nc.vector.memset(ks_pool[:].bitcast(I32), 0)
+        nc.gpsimd.memset(ks_pool[:].bitcast(I32), 0)
         nc.vector.memset(vs_pool[:], 0.0)
 
         xq_planes = xq.rearrange("(p t) n -> p t n", t=PACK)
         ks_rows = k_scales[0].bitcast(I32)
         nc.sync.dma_start(xq_pool[0][:], xq_planes[:, 0, :])
+        nc.sync.dma_start(slot_list[:], offs)
+        nc.sync.dma_start(ks_pool[0:P:KS_STEP, :].bitcast(I32), ks_rows)
         nc.sync.dma_start(query_list[:], qoffs)
         nc.sync.dma_start(xq_pool[1][:], xq_planes[:, 1, :])
-        nc.sync.dma_start(slot_list[:], offs)
-        for r in range(4):
-            nc.sync.dma_start(ks_pool[r:P:32, :].bitcast(I32), ks_rows[r:16:4, :])
         nc.sync.dma_start(vs_pool[VS_ROW : VS_ROW + 1, :], vs[0:1, :])
         nc.sync.dma_start(xq_pool[2][:], xq_planes[:, 2, :])
         nc.sync.dma_start(xq_pool[3][:], xq_planes[:, 3, :])
-        nc.sync.dma_start(kw_pool[:], k_words[0].rearrange("p n t -> p (n t)").bitcast(I32))
-        for h in range(EB):
-            nc.sync.dma_start(v_pool[h][:], vT[h * P : (h + 1) * P, :])
 
         ident = sb.tile([P, P], F32, name="ident")
         make_identity(nc, ident[:])
@@ -71,13 +68,24 @@ def tile_attend_router_kernel(tc, xq, k_words, k_scales, vT, vs, offs, qoffs, ou
         def gather_queries(t):
             nc.vector.tensor_copy(q_bf[:, :, t], xq_pool[t][:].indirect(query_list[:]))
 
-        gather_queries(0)
-        gather_queries(1)
-
         k_codes = sb.tile([P, N], U32, name="k_codes", align_bytes=64)
         k_bytes = sb.tile([P, N], U8, name="k_bytes", align_bytes=64)
         vs_row = sb.tile([P, N], F32, name="vs_row")
-        nc.vector.tensor_copy(k_bytes[:], ks_pool[:].indirect(slot_list[:]))
+        ks_picked = sb.tile([P, N], U8, name="ks_picked")
+        nc.vector.memset(k_bytes[:].bitcast(I32), 0)
+        nc.vector.tensor_copy(ks_picked[:], ks_pool[:].indirect(slot_list[:]))
+        for r in range(4):
+            nc.sync.dma_start(k_bytes[r:P:32, :].bitcast(I32), ks_picked[r * KS_STEP : P : 32, :].bitcast(I32))
+        kw_pool = sb.tile([P, T], I32, name="kw_pool", tag="keys")
+        nc.sync.dma_start(kw_pool[:], k_words[0].rearrange("p n t -> p (n t)").bitcast(I32))
+
+        gather_queries(0)
+        v_pool = [sb.tile([P, T], F32, name="v_pool0", tag="first")]
+        nc.sync.dma_start(v_pool[0][:], vT[0:P, :])
+        gather_queries(1)
+        v_pool.append(late.tile([P, T], F32, name="v_pool1", align_bytes=64, offset=0))
+        nc.sync.dma_start(v_pool[1][:], vT[P : 2 * P, :])
+
         nc.vector.tensor_copy(vs_row[:], vs_pool[:].indirect(slot_list[:]))
 
         vs_ps = ps.tile([P, PACK, P], F32, name="vs_ps", tag="aux")
@@ -132,10 +140,16 @@ def tile_attend_router_kernel(tc, xq, k_words, k_scales, vT, vs, offs, qoffs, ou
                 nc.tensor.transpose(pt[:, t, :], probs[b][:, t, :], ident[:])
             p_turned.append(pt)
 
-        v_codes = [late.tile([P, P], U32, name="v_codes0", align_bytes=64, offset=0),
-                   sb.tile([P, P], U32, name="v_codes1", align_bytes=64)]
-        v_bytes = [sb.tile([P, P], U8, name=f"v_bytes{h}", align_bytes=64) for h in range(EB)]
-        v_bf = [sb.tile([P, P * PACK], BF16, name=f"v_bf{h}", align_bytes=64) for h in range(EB)]
+        early_bf = sb.tile([P, 2, N], BF16, name="early_bf", align_bytes=64)
+        v1_bf = sb.tile([P, N], BF16, name="v1_bf", align_bytes=64)
+        w1_bf = late.tile([P, P, PACK], BF16, name="w1_bf", align_bytes=64, offset=0)
+        codes = late.tile([P, 3 * P], U32, name="codes", align_bytes=64, offset=1024)
+        scales = sb.tile([P, 3 * P], U8, name="scales", align_bytes=64)
+        v1_codes = sb.tile([P, P], U32, name="v1_codes", align_bytes=64)
+        v1_scales = sb.tile([P, P], U8, name="v1_scales", align_bytes=64)
+        v_bf = [early_bf[:, 0, :], v1_bf[:]]
+        v_codes = [codes[:, 0:P], v1_codes[:]]
+        v_scales = [scales[:, 0:P], v1_scales[:]]
 
         def turn_values(h):
             picked = sb.tile([P, 2, P, 2], BF16, name=f"v_picked{h}")
@@ -144,34 +158,18 @@ def tile_attend_router_kernel(tc, xq, k_words, k_scales, vT, vs, offs, qoffs, ou
             vt = ps.tile([P, 2, P], F32, name=f"vt{h}", tag="vt")
             for u in range(2):
                 nc.tensor.transpose(vt[:, u, :], pairs[:, u * P : (u + 1) * P], ident[:])
-            nc.scalar.copy(v_bf[h][:].bitcast(F32).rearrange("s (r u) -> s r u", u=2), vt[:].rearrange("s u r -> s r u"))
+            nc.scalar.copy(v_bf[h].bitcast(F32).rearrange("s (r u) -> s r u", u=2), vt[:].rearrange("s u r -> s r u"))
 
-        def quantize_values(h):
-            nc.vector.quantize_mx(out=v_codes[h][:].bitcast(FP8X4), scales=v_bytes[h][:], in_=v_bf[h][:])
-
-        w_bf = [sb.tile([P, P, PACK], BF16, name="w_bf0", align_bytes=64),
-                late.tile([P, P, PACK], BF16, name="w_bf1", align_bytes=64, offset=512)]
-        w_codes = late.tile([P, NQ], U32, name="w_codes", align_bytes=64, offset=1536)
-        w_bytes = sb.tile([P, NQ], U8, name="w_bytes", align_bytes=64)
-        vs_wide = vs_col[:].unsqueeze(1).to_broadcast([P, P, PACK])
-
-        def weigh(b):
-            nc.vector.tensor_tensor(w_bf[b][:], p_turned[b][:].rearrange("s t q -> s q t"), vs_wide, ALU.mult)
-
-        def quantize_weights(b):
-            cols = slice(b * P, (b + 1) * P)
-            nc.vector.quantize_mx(out=w_codes[:, cols].bitcast(FP8X4), scales=w_bytes[:, cols],
-                                  in_=w_bf[b][:].rearrange("s q t -> s (q t)"))
-
-        inv_sum = late.tile([P, QB], F32, name="inv_sum", align_bytes=64, offset=3584)
+        inv_sum = sb.tile([P, QB], F32, name="inv_sum")
         inv_wide = late.tile([P, NQ], F32, name="inv_wide", align_bytes=64, offset=2560)
         y_sb = [sb.tile([P, NQ], F32, name=f"y_sb{h}") for h in range(EB)]
 
-        def product(h, cols, tag):
-            y = ps.tile([P, cols.stop - cols.start], F32, name=f"y_{tag}", tag=tag)
-            nc.tensor.matmul_mx(out=y[:], lhsT=v_codes[h][:].bitcast(FP8X4), lhsT_scale=v_bytes[h][:],
-                                rhs=w_codes[:, cols].bitcast(FP8X4), rhs_scale=w_bytes[:, cols], start=True, stop=True)
-            nc.scalar.copy(y_sb[h][:, cols], y[:])
+        def product(h, first, last, tag):
+            cols = slice(P + first, P + last)
+            y = ps.tile([P, last - first], F32, name=f"y_{tag}", tag=tag)
+            nc.tensor.matmul_mx(out=y[:], lhsT=v_codes[h].bitcast(FP8X4), lhsT_scale=v_scales[h],
+                                rhs=codes[:, cols].bitcast(FP8X4), rhs_scale=scales[:, cols], start=True, stop=True)
+            nc.scalar.copy(y_sb[h][:, first:last], y[:])
 
         def finish(h):
             nc.vector.tensor_tensor(result[h][:].indirect(query_list[:]), y_sb[h][:], inv_wide[:], ALU.mult)
@@ -182,20 +180,24 @@ def tile_attend_router_kernel(tc, xq, k_words, k_scales, vT, vs, offs, qoffs, ou
         for t in range(PACK):
             nc.scalar.activation(w_planes[:, t, :], p_turned[0][:, t, :], ACT.Copy, scale=vs_col[:, t : t + 1])
         turn_values(0)
-        nc.scalar.copy(w_bf[0][:].rearrange("s (c i) t -> s c t i", i=4), w_planes[:].rearrange("s t (c i) -> s c t i", i=4))
+        nc.scalar.copy(early_bf[:, 1, :].rearrange("s (c i t) -> s c t i", i=4, t=PACK),
+                       w_planes[:].rearrange("s t (c i) -> s c t i", i=4))
         turn_weights(1)
         turn_values(1)
-        weigh(1)
+        nc.vector.tensor_tensor(w1_bf[:], p_turned[1][:].rearrange("s t q -> s q t"),
+                                vs_col[:].unsqueeze(1).to_broadcast([P, P, PACK]), ALU.mult)
         nc.vector.reciprocal(inv_sum[:], row_sum[:])
         inv_ps = ps.tile([P, QB, P], F32, name="inv_ps", tag="aux")
         for b in range(QB):
             nc.tensor.transpose(inv_ps[:, b, :], inv_sum[:, b : b + 1].to_broadcast([P, P]), ident[:])
-        quantize_values(0)
-        for b in reversed(range(QB)):
-            quantize_weights(b)
-            product(0, slice(b * P, (b + 1) * P), f"acc0_{b}")
-        quantize_values(1)
+        nc.vector.quantize_mx(out=codes[:, 0 : 2 * P].bitcast(FP8X4), scales=scales[:, 0 : 2 * P],
+                              in_=early_bf[:].rearrange("s a n -> s (a n)"))
+        product(0, 0, P, "acc0_0")
+        nc.vector.quantize_mx(out=codes[:, 2 * P : 3 * P].bitcast(FP8X4), scales=scales[:, 2 * P : 3 * P],
+                              in_=w1_bf[:].rearrange("s q t -> s (q t)"))
+        product(0, P, NQ, "acc0_1")
+        nc.vector.quantize_mx(out=v1_codes[:].bitcast(FP8X4), scales=v1_scales[:], in_=v1_bf[:])
         nc.vector.tensor_copy(inv_wide[:], inv_ps[:].rearrange("p b q -> p (b q)"))
-        product(1, slice(0, NQ), "acc1_0")
+        product(1, 0, NQ, "acc1_0")
         finish(0)
         finish(1)

@@ -72,9 +72,9 @@ def tile_attend_router_kernel(tc, xq, k_words, k_scales, vT, vs, offs, qoffs, ou
         k_bytes = sb.tile([P, N], U8, name="k_bytes", align_bytes=64)
         vs_row = sb.tile([P, N], F32, name="vs_row")
         ks_picked = sb.tile([P, N], U8, name="ks_picked")
-        nc.vector.memset(k_bytes[:].bitcast(I32), 0)
         nc.vector.tensor_copy(ks_picked[:], ks_pool[:].indirect(slot_list[:]))
-        for r in range(4):
+        nc.vector.tensor_copy(k_bytes[:].bitcast(I32), ks_picked[:].bitcast(I32))
+        for r in range(1, 4):
             nc.sync.dma_start(k_bytes[r:P:32, :].bitcast(I32), ks_picked[r * KS_STEP : P : 32, :].bitcast(I32))
         kw_pool = sb.tile([P, T], I32, name="kw_pool", tag="keys")
         nc.sync.dma_start(kw_pool[:], k_words[0].rearrange("p n t -> p (n t)").bitcast(I32))

@@ -12,15 +12,15 @@ U8 = mybir.dt.uint8
 FP8X4 = mybir.dt.float8_e4m3fn_x4
 ACT = mybir.ActivationFunctionType
 ALU = mybir.AluOpType
-AX = mybir.AxisListType
 
 P = 128
 PACK = 4
 T, D, DV, N, NQ = 2048, 512, 256, 512, 256
 QB = NQ // P
 EB = DV // P
+HALF = N // 2
+SCALE_STEP = P // (D // 32)
 VS_ROW = 4
-KS_STEP = 8
 
 FLOPS = 2 * NQ * N * (D + DV)
 BYTES = 4 * D * T + D * T + (D // 32) * T + 4 * DV * T + 4 * T + 2 * P * (N + NQ) // 16 + 4 * DV * T
@@ -30,26 +30,25 @@ def tile_attend_router_kernel(tc, xq, k_words, k_scales, vT, vs, offs, qoffs, ou
     nc = tc.nc
     with ExitStack() as ctx:
         sb = ctx.enter_context(tc.tile_pool(name="sb", bufs=1))
-        late = ctx.enter_context(tc.tile_pool(name="late", bufs=1))
+        reused = ctx.enter_context(tc.tile_pool(name="reused", bufs=1))
         ps = ctx.enter_context(tc.psum_pool(name="ps", bufs=1))
 
         slot_list = sb.tile([P, N // 16], U16, name="slot_list")
         query_list = sb.tile([P, NQ // 16], U16, name="query_list")
-        xq_pool = [sb.tile([P, T], F32, name="xq_pool0", tag="first"),
-                   late.tile([P, T], F32, name="xq_pool1", align_bytes=64, offset=0),
+        xq_pool = [sb.tile([P, T], F32, name="xq_pool0", tag="xq0_then_v0"),
+                   reused.tile([P, T], F32, name="xq_pool1", align_bytes=64, offset=0),
                    sb.tile([P, T], F32, name="xq_pool2"), sb.tile([P, T], F32, name="xq_pool3")]
-        ks_pool = sb.tile([P, T], U8, name="ks_pool", tag="keys")
+        ks_pool = sb.tile([P, T], U8, name="ks_pool", tag="scales_then_words")
         vs_pool = sb.tile([P, T], F32, name="vs_pool")
         result = [sb.tile([P, T], F32, name=f"result{h}") for h in range(EB)]
 
         nc.gpsimd.memset(ks_pool[:].bitcast(I32), 0)
         nc.vector.memset(vs_pool[:], 0.0)
 
-        xq_planes = xq.rearrange("(p t) n -> p t n", t=PACK)
-        ks_rows = k_scales[0].bitcast(I32)
+        xq_planes = xq.rearrange("(s t) n -> s t n", t=PACK)
         nc.sync.dma_start(xq_pool[0][:], xq_planes[:, 0, :])
         nc.sync.dma_start(slot_list[:], offs)
-        nc.sync.dma_start(ks_pool[0:P:KS_STEP, :].bitcast(I32), ks_rows)
+        nc.sync.dma_start(ks_pool[0:P:SCALE_STEP, :].bitcast(I32), k_scales[0].bitcast(I32))
         nc.sync.dma_start(query_list[:], qoffs)
         nc.sync.dma_start(xq_pool[1][:], xq_planes[:, 1, :])
         nc.sync.dma_start(vs_pool[VS_ROW : VS_ROW + 1, :], vs[0:1, :])
@@ -58,8 +57,6 @@ def tile_attend_router_kernel(tc, xq, k_words, k_scales, vT, vs, offs, qoffs, ou
 
         ident = sb.tile([P, P], F32, name="ident")
         make_identity(nc, ident[:])
-        warm = sb.tile([P, 1], F32, name="warm")
-        nc.scalar.activation(warm[:], ident[:, 0:1], ACT.Exp)
         for h in range(EB):
             nc.gpsimd.memset(result[h][:], 0.0)
 
@@ -75,129 +72,140 @@ def tile_attend_router_kernel(tc, xq, k_words, k_scales, vT, vs, offs, qoffs, ou
         nc.vector.tensor_copy(ks_picked[:], ks_pool[:].indirect(slot_list[:]))
         nc.vector.tensor_copy(k_bytes[:].bitcast(I32), ks_picked[:].bitcast(I32))
         for r in range(1, 4):
-            nc.sync.dma_start(k_bytes[r:P:32, :].bitcast(I32), ks_picked[r * KS_STEP : P : 32, :].bitcast(I32))
-        kw_pool = sb.tile([P, T], I32, name="kw_pool", tag="keys")
-        nc.sync.dma_start(kw_pool[:], k_words[0].rearrange("p n t -> p (n t)").bitcast(I32))
+            nc.sync.dma_start(k_bytes[r:P:32, :].bitcast(I32), ks_picked[r * SCALE_STEP : P : 32, :].bitcast(I32))
 
+        kw_pool = sb.tile([P, T], I32, name="kw_pool", tag="scales_then_words")
+        nc.sync.dma_start(kw_pool[:], k_words[0].rearrange("s n t -> s (n t)").bitcast(I32))
         gather_queries(0)
-        v_pool = [sb.tile([P, T], F32, name="v_pool0", tag="first")]
+        v_pool = [sb.tile([P, T], F32, name="v_pool0", tag="xq0_then_v0")]
         nc.sync.dma_start(v_pool[0][:], vT[0:P, :])
         gather_queries(1)
-        v_pool.append(late.tile([P, T], F32, name="v_pool1", align_bytes=64, offset=0))
+        v_pool.append(reused.tile([P, T], F32, name="v_pool1", align_bytes=64, offset=0))
         nc.sync.dma_start(v_pool[1][:], vT[P : 2 * P, :])
 
         nc.vector.tensor_copy(vs_row[:], vs_pool[:].indirect(slot_list[:]))
-
-        vs_ps = ps.tile([P, PACK, P], F32, name="vs_ps", tag="aux")
+        vs_turned = ps.tile([P, PACK, P], F32, name="vs_turned", tag="rows")
         for t in range(PACK):
-            nc.tensor.transpose(vs_ps[:, t, :], vs_row[:, t : N : PACK], ident[:])
+            nc.tensor.transpose(vs_turned[:, t, :], vs_row[:, t:N:PACK], ident[:])
         vs_col = sb.tile([P, PACK], F32, name="vs_col")
-        nc.scalar.copy(vs_col[:], vs_ps[:, :, VS_ROW])
+        nc.scalar.copy(vs_col[:], vs_turned[:, :, VS_ROW])
+        vs_wide = ps.tile([P, PACK, P], F32, name="vs_wide", tag="rows")
+        for t in range(PACK):
+            nc.tensor.transpose(vs_wide[:, t, :], vs_col[:, t : t + 1].to_broadcast([P, P]), ident[:])
 
         gather_queries(2)
         gather_queries(3)
 
         q_codes = sb.tile([P, NQ], U32, name="q_codes", align_bytes=64)
         q_bytes = sb.tile([P, NQ], U8, name="q_bytes", align_bytes=64)
-        q_flat = q_bf[:].rearrange("p q t -> p (q t)")
-        scores = []
+        q_flat = q_bf[:].rearrange("s q t -> s (q t)")
         for b in range(QB):
             cols = slice(b * P, (b + 1) * P)
             nc.vector.quantize_mx(out=q_codes[:, cols].bitcast(FP8X4), scales=q_bytes[:, cols],
                                   in_=q_flat[:, b * P * PACK : (b + 1) * P * PACK])
-        half = N // 2
-        for b in range(QB):
-            scores.append([ps.tile([P, half], F32, name=f"score{b}_{j}", tag=f"acc{b}_{j}") for j in range(2)])
+
+        scores = [[ps.tile([P, HALF], F32, name=f"score{b}_{j}", tag=f"bank{b}_{j}") for j in range(2)]
+                  for b in range(QB)]
         for j in range(2):
-            slots = slice(j * half, (j + 1) * half)
+            slots = slice(j * HALF, (j + 1) * HALF)
             nc.vector.tensor_copy(k_codes[:, slots],
-                                  kw_pool[:].bitcast(U32).indirect(slot_list[:, j * half // 16 : (j + 1) * half // 16]))
+                                  kw_pool[:].bitcast(U32).indirect(slot_list[:, j * HALF // 16 : (j + 1) * HALF // 16]))
             for b in range(QB):
                 cols = slice(b * P, (b + 1) * P)
                 nc.tensor.matmul_mx(out=scores[b][j][:], lhsT=q_codes[:, cols].bitcast(FP8X4), lhsT_scale=q_bytes[:, cols],
                                     rhs=k_codes[:, slots].bitcast(FP8X4), rhs_scale=k_bytes[:, slots], start=True, stop=True)
 
-        row_sum = sb.tile([P, QB], F32, name="row_sum")
-        p_turned = []
-        probs = []
-        neg_score = [sb.tile([P, PACK, P], F32, name=f"neg_score{b}") for b in range(QB)]
+        neg_score0 = sb.tile([P, PACK, P], F32, name="neg_score0")
+        neg_score1 = sb.tile([P, 2, P, 2], F32, name="neg_score1")
         neg_max = [[sb.tile([P, 1], F32, name=f"neg_max{b}_{j}") for j in range(2)] for b in range(QB)]
         for j in range(2):
-            for b in range(QB):
-                nc.vector.tensor_scalar(neg_score[b][:, :, j * P // 2 : (j + 1) * P // 2],
-                                        scores[b][j][:].rearrange("q (s t) -> q t s", t=PACK),
-                                        -1.0, neg_max[b][0][:] if j else None, ALU.mult, ALU.min,
+            s_half = slice(j * P // 2, (j + 1) * P // 2)
+            laid_out = [(neg_score0[:, :, s_half], scores[0][j][:].rearrange("q (s t) -> q t s", t=PACK)),
+                        (neg_score1[:, :, s_half, :], scores[1][j][:].rearrange("q (s u e) -> q u s e", u=2, e=2))]
+            for b, (dst, src) in enumerate(laid_out):
+                nc.vector.tensor_scalar(dst, src, -1.0, neg_max[b][0][:] if j else None, ALU.mult, ALU.min,
                                         accum_out=neg_max[b][j][:])
-        for b in range(QB):
-            p = sb.tile([P, PACK, P], F32, name=f"p{b}")
-            nc.scalar.activation(p[:], neg_score[b][:], ACT.Exp, scale=-1.0,
-                                 bias=neg_max[b][1][:], accum_out=row_sum[:, b : b + 1])
-            probs.append(p)
 
-        def turn_weights(b):
-            pt = ps.tile([P, PACK, P], F32, name=f"pt{b}")
-            for t in range(PACK):
-                nc.tensor.transpose(pt[:, t, :], probs[b][:, t, :], ident[:])
-            p_turned.append(pt)
+        sum_parts = sb.tile([P, 2, QB], F32, name="sum_parts")
+        p0 = [sb.tile([P, 2, P], F32, name=f"p0_{u}") for u in range(2)]
+        for u in range(2):
+            nc.scalar.activation(p0[u][:], neg_score0[:, 2 * u : 2 * u + 2, :], ACT.Exp, scale=-1.0,
+                                 bias=neg_max[0][1][:], accum_out=sum_parts[:, u, 0:1])
+        p1 = [sb.tile([P, P, 2], F32, name=f"p1_{u}") for u in range(2)]
+        for u in range(2):
+            nc.scalar.activation(p1[u][:], neg_score1[:, u, :, :], ACT.Exp, scale=-1.0,
+                                 bias=neg_max[1][1][:], accum_out=sum_parts[:, u, 1:2])
+        row_sum = sb.tile([P, QB], F32, name="row_sum")
+        nc.gpsimd.tensor_tensor(row_sum[:], sum_parts[:, 0, :], sum_parts[:, 1, :], ALU.add)
 
-        early_bf = sb.tile([P, 2, N], BF16, name="early_bf", align_bytes=64)
+        vw0_bf = sb.tile([P, 2, N], BF16, name="vw0_bf", align_bytes=64)
         v1_bf = sb.tile([P, N], BF16, name="v1_bf", align_bytes=64)
-        w1_bf = late.tile([P, P, PACK], BF16, name="w1_bf", align_bytes=64, offset=0)
-        codes = late.tile([P, 3 * P], U32, name="codes", align_bytes=64, offset=1024)
+        w1_bf = sb.tile([P, N], BF16, name="w1_bf", align_bytes=64)
+        codes = reused.tile([P, 3 * P], U32, name="codes", align_bytes=64, offset=0)
         scales = sb.tile([P, 3 * P], U8, name="scales", align_bytes=64)
         v1_codes = sb.tile([P, P], U32, name="v1_codes", align_bytes=64)
         v1_scales = sb.tile([P, P], U8, name="v1_scales", align_bytes=64)
-        v_bf = [early_bf[:, 0, :], v1_bf[:]]
+        v_bf = [vw0_bf[:, 0, :], v1_bf[:]]
         v_codes = [codes[:, 0:P], v1_codes[:]]
         v_scales = [scales[:, 0:P], v1_scales[:]]
 
         def turn_values(h):
             picked = sb.tile([P, 2, P, 2], BF16, name=f"v_picked{h}")
-            nc.vector.tensor_copy(picked[:].rearrange("p u s e -> p s u e"), v_pool[h][:].indirect(slot_list[:]))
-            pairs = picked[:].rearrange("p u s e -> p (u s e)").bitcast(F32)
-            vt = ps.tile([P, 2, P], F32, name=f"vt{h}", tag="vt")
+            nc.vector.tensor_copy(picked[:].rearrange("f u s e -> f s u e"), v_pool[h][:].indirect(slot_list[:]))
+            pairs = picked[:].rearrange("f u s e -> f (u s e)").bitcast(F32)
+            v_turned = ps.tile([P, 2, P], F32, name=f"v_turned{h}", tag="v_turned")
             for u in range(2):
-                nc.tensor.transpose(vt[:, u, :], pairs[:, u * P : (u + 1) * P], ident[:])
-            nc.scalar.copy(v_bf[h].bitcast(F32).rearrange("s (r u) -> s r u", u=2), vt[:].rearrange("s u r -> s r u"))
+                nc.tensor.transpose(v_turned[:, u, :], pairs[:, u * P : (u + 1) * P], ident[:])
+            nc.scalar.copy(v_bf[h].bitcast(F32).rearrange("s (f u) -> s f u", u=2), v_turned[:].rearrange("s u f -> s f u"))
 
         inv_sum = sb.tile([P, QB], F32, name="inv_sum")
-        inv_wide = late.tile([P, NQ], F32, name="inv_wide", align_bytes=64, offset=2560)
+        inv_wide = reused.tile([P, NQ], F32, name="inv_wide", align_bytes=64, offset=4 * 3 * P)
         y_sb = [sb.tile([P, NQ], F32, name=f"y_sb{h}") for h in range(EB)]
 
-        def product(h, first, last, tag):
+        def product(h, first, last, bank):
             cols = slice(P + first, P + last)
-            y = ps.tile([P, last - first], F32, name=f"y_{tag}", tag=tag)
+            y = ps.tile([P, last - first], F32, name=f"y_{bank}", tag=bank)
             nc.tensor.matmul_mx(out=y[:], lhsT=v_codes[h].bitcast(FP8X4), lhsT_scale=v_scales[h],
                                 rhs=codes[:, cols].bitcast(FP8X4), rhs_scale=scales[:, cols], start=True, stop=True)
             nc.scalar.copy(y_sb[h][:, first:last], y[:])
 
-        def finish(h):
+        w_planes = sb.tile([P, PACK, P], BF16, name="w_planes")
+        for u in range(2):
+            p_turned = ps.tile([P, 2, P], F32, name=f"p_turned{u}", tag=f"bank0_{u}")
+            for e in range(2):
+                nc.tensor.transpose(p_turned[:, e, :], p0[u][:, e, :], ident[:])
+            for e in range(2):
+                t = 2 * u + e
+                nc.scalar.activation(w_planes[:, t, :], p_turned[:, e, :], ACT.Copy, scale=vs_col[:, t : t + 1])
+        turn_values(0)
+        nc.scalar.copy(vw0_bf[:, 1, :].rearrange("s (c i t) -> s c t i", i=4, t=PACK),
+                       w_planes[:].rearrange("s t (c i) -> s c t i", i=4))
+
+        w_turned = ps.tile([P, 2, P], F32, name="w_turned")
+        for u in range(2):
+            w_pairs = sb.tile([P, P, 2], BF16, name=f"w_pairs{u}")
+            nc.vector.tensor_tensor(w_pairs[:], vs_wide[:, 2 * u : 2 * u + 2, :].rearrange("q e s -> q s e"),
+                                    p1[u][:], ALU.mult)
+            nc.tensor.transpose(w_turned[:, u, :], w_pairs[:].rearrange("q s e -> q (s e)").bitcast(F32), ident[:])
+        nc.scalar.copy(w1_bf[:].bitcast(F32).rearrange("s (q u) -> s q u", u=2), w_turned[:].rearrange("s u q -> s q u"))
+        turn_values(1)
+
+        minus_one = sb.tile([P, QB], F32, name="minus_one")
+        nc.gpsimd.memset(minus_one[:], -1.0)
+        nc.gpsimd.tensor_tensor(inv_sum[:], row_sum[:], minus_one[:], ALU.pow)
+        inv_turned = ps.tile([P, QB, P], F32, name="inv_turned", tag="rows")
+        for b in range(QB):
+            nc.tensor.transpose(inv_turned[:, b, :], inv_sum[:, b : b + 1].to_broadcast([P, P]), ident[:])
+
+        nc.vector.quantize_mx(out=codes[:, 0 : 2 * P].bitcast(FP8X4), scales=scales[:, 0 : 2 * P],
+                              in_=vw0_bf[:].rearrange("s a n -> s (a n)"))
+        product(0, 0, P, "bank0_0")
+        nc.vector.quantize_mx(out=codes[:, 2 * P : 3 * P].bitcast(FP8X4), scales=scales[:, 2 * P : 3 * P], in_=w1_bf[:])
+        product(0, P, NQ, "bank0_1")
+        nc.vector.tensor_copy(inv_wide[:], inv_turned[:].rearrange("f b q -> f (b q)"))
+        nc.vector.quantize_mx(out=v1_codes[:].bitcast(FP8X4), scales=v1_scales[:], in_=v1_bf[:])
+        product(1, 0, NQ, "bank1_0")
+
+        for h in range(EB):
             nc.vector.tensor_tensor(result[h][:].indirect(query_list[:]), y_sb[h][:], inv_wide[:], ALU.mult)
             nc.sync.dma_start(out[h * P : (h + 1) * P, :], result[h][:])
-
-        turn_weights(0)
-        w_planes = sb.tile([P, PACK, P], BF16, name="w_planes")
-        for t in range(PACK):
-            nc.scalar.activation(w_planes[:, t, :], p_turned[0][:, t, :], ACT.Copy, scale=vs_col[:, t : t + 1])
-        turn_values(0)
-        nc.scalar.copy(early_bf[:, 1, :].rearrange("s (c i t) -> s c t i", i=4, t=PACK),
-                       w_planes[:].rearrange("s t (c i) -> s c t i", i=4))
-        turn_weights(1)
-        turn_values(1)
-        nc.vector.tensor_tensor(w1_bf[:], p_turned[1][:].rearrange("s t q -> s q t"),
-                                vs_col[:].unsqueeze(1).to_broadcast([P, P, PACK]), ALU.mult)
-        nc.vector.reciprocal(inv_sum[:], row_sum[:])
-        inv_ps = ps.tile([P, QB, P], F32, name="inv_ps", tag="aux")
-        for b in range(QB):
-            nc.tensor.transpose(inv_ps[:, b, :], inv_sum[:, b : b + 1].to_broadcast([P, P]), ident[:])
-        nc.vector.quantize_mx(out=codes[:, 0 : 2 * P].bitcast(FP8X4), scales=scales[:, 0 : 2 * P],
-                              in_=early_bf[:].rearrange("s a n -> s (a n)"))
-        product(0, 0, P, "acc0_0")
-        nc.vector.quantize_mx(out=codes[:, 2 * P : 3 * P].bitcast(FP8X4), scales=scales[:, 2 * P : 3 * P],
-                              in_=w1_bf[:].rearrange("s q t -> s (q t)"))
-        product(0, P, NQ, "acc0_1")
-        nc.vector.quantize_mx(out=v1_codes[:].bitcast(FP8X4), scales=v1_scales[:], in_=v1_bf[:])
-        nc.vector.tensor_copy(inv_wide[:], inv_ps[:].rearrange("p b q -> p (b q)"))
-        product(1, 0, NQ, "acc1_0")
-        finish(0)
-        finish(1)

@@ -12,6 +12,7 @@ U8 = mybir.dt.uint8
 FP8X4 = mybir.dt.float8_e4m3fn_x4
 ACT = mybir.ActivationFunctionType
 ALU = mybir.AluOpType
+AX = mybir.AxisListType
 
 P = 128
 PACK = 4
@@ -123,8 +124,11 @@ def tile_attend_router_kernel(tc, xq, k_words, k_scales, vT, vs, offs, qoffs, ou
             laid_out = [(neg_score0[:, :, s_half], scores[0][j][:].rearrange("q (s t) -> q t s", t=PACK)),
                         (neg_score1[:, :, s_half, :], scores[1][j][:].rearrange("q (s u e) -> q u s e", u=2, e=2))]
             for b, (dst, src) in enumerate(laid_out):
-                nc.vector.tensor_scalar(dst, src, -1.0, neg_max[b][0][:] if j else None, ALU.mult, ALU.min,
-                                        accum_out=neg_max[b][j][:])
+                if j == 0:
+                    nc.vector.tensor_reduce(neg_max[b][0][:], scores[b][0][:], AX.X, ALU.max, negate=True)
+                    nc.scalar.activation(dst, src, ACT.Copy, scale=-1.0)
+                else:
+                    nc.vector.tensor_scalar(dst, src, -1.0, neg_max[b][0][:], ALU.mult, ALU.min, accum_out=neg_max[b][1][:])
 
         sum_parts = sb.tile([P, 2, QB], F32, name="sum_parts")
         p0 = [sb.tile([P, 2, P], F32, name=f"p0_{u}") for u in range(2)]

@@ -94,6 +94,9 @@ def tile_attend_router_kernel(tc, xq, k_words, k_scales, vT, vs, offs, qoffs, ou
         for t in range(PACK):
             nc.tensor.transpose(vs_wide[:, t, :], vs_col[:, t : t + 1].to_broadcast([P, P]), ident[:])
 
+        vs_pairs = sb.tile([P, 2, P, 2], F32, name="vs_pairs")
+        nc.scalar.copy(vs_pairs[:], vs_wide[:].rearrange("q (u e) s -> q u s e", e=2))
+
         gather_queries(2)
         gather_queries(3)
 
@@ -116,14 +119,13 @@ def tile_attend_router_kernel(tc, xq, k_words, k_scales, vT, vs, offs, qoffs, ou
                 nc.tensor.matmul_mx(out=scores[b][j][:], lhsT=q_codes[:, cols].bitcast(FP8X4), lhsT_scale=q_bytes[:, cols],
                                     rhs=k_codes[:, slots].bitcast(FP8X4), rhs_scale=k_bytes[:, slots], start=True, stop=True)
 
-        neg_score0 = sb.tile([P, PACK, P], F32, name="neg_score0")
-        neg_score1 = sb.tile([P, 2, P, 2], F32, name="neg_score1")
+        neg_score = [sb.tile([P, 2, P, 2], F32, name=f"neg_score{b}") for b in range(QB)]
         neg_max = [[sb.tile([P, 1], F32, name=f"neg_max{b}_{j}") for j in range(2)] for b in range(QB)]
         for j in range(2):
             s_half = slice(j * P // 2, (j + 1) * P // 2)
-            laid_out = [(neg_score0[:, :, s_half], scores[0][j][:].rearrange("q (s t) -> q t s", t=PACK)),
-                        (neg_score1[:, :, s_half, :], scores[1][j][:].rearrange("q (s u e) -> q u s e", u=2, e=2))]
-            for b, (dst, src) in enumerate(laid_out):
+            for b in range(QB):
+                dst = neg_score[b][:, :, s_half, :]
+                src = scores[b][j][:].rearrange("q (s u e) -> q u s e", u=2, e=2)
                 if j == 0:
                     nc.vector.tensor_reduce(neg_max[b][0][:], scores[b][0][:], AX.X, ALU.max, negate=True)
                     nc.scalar.activation(dst, src, ACT.Copy, scale=-1.0)
@@ -131,16 +133,15 @@ def tile_attend_router_kernel(tc, xq, k_words, k_scales, vT, vs, offs, qoffs, ou
                     nc.vector.tensor_scalar(dst, src, -1.0, neg_max[b][0][:], ALU.mult, ALU.min, accum_out=neg_max[b][1][:])
 
         sum_parts = sb.tile([P, 2, QB], F32, name="sum_parts")
-        p0 = [sb.tile([P, 2, P], F32, name=f"p0_{u}") for u in range(2)]
-        for u in range(2):
-            nc.scalar.activation(p0[u][:], neg_score0[:, 2 * u : 2 * u + 2, :], ACT.Exp, scale=-1.0,
-                                 bias=neg_max[0][1][:], accum_out=sum_parts[:, u, 0:1])
-        p1 = [sb.tile([P, P, 2], F32, name=f"p1_{u}") for u in range(2)]
-        for u in range(2):
-            nc.scalar.activation(p1[u][:], neg_score1[:, u, :, :], ACT.Exp, scale=-1.0,
-                                 bias=neg_max[1][1][:], accum_out=sum_parts[:, u, 1:2])
+        p = [[sb.tile([P, P, 2], F32, name=f"p{b}_{u}") for u in range(2)] for b in range(QB)]
+        for b in range(QB):
+            for u in range(2):
+                nc.scalar.activation(p[b][u][:], neg_score[b][:, u, :, :], ACT.Exp, scale=-1.0,
+                                     bias=neg_max[b][1][:], accum_out=sum_parts[:, u, b : b + 1])
         row_sum = sb.tile([P, QB], F32, name="row_sum")
-        nc.gpsimd.tensor_tensor(row_sum[:], sum_parts[:, 0, :], sum_parts[:, 1, :], ALU.add)
+        for b in range(QB):
+            nc.scalar.activation(row_sum[:, b : b + 1], sum_parts[:, 0, b : b + 1], ACT.Identity,
+                                 bias=sum_parts[:, 1, b : b + 1])
 
         vw0_bf = sb.tile([P, 2, N], BF16, name="vw0_bf", align_bytes=64)
         v1_bf = sb.tile([P, N], BF16, name="v1_bf", align_bytes=64)
@@ -173,25 +174,21 @@ def tile_attend_router_kernel(tc, xq, k_words, k_scales, vT, vs, offs, qoffs, ou
                                 rhs=codes[:, cols].bitcast(FP8X4), rhs_scale=scales[:, cols], start=True, stop=True)
             nc.scalar.copy(y_sb[h][:, first:last], y[:])
 
-        w_planes = sb.tile([P, PACK, P], BF16, name="w_planes")
-        for u in range(2):
-            p_turned = ps.tile([P, 2, P], F32, name=f"p_turned{u}", tag=f"bank0_{u}")
-            for e in range(2):
-                nc.tensor.transpose(p_turned[:, e, :], p0[u][:, e, :], ident[:])
-            for e in range(2):
-                t = 2 * u + e
-                nc.scalar.activation(w_planes[:, t, :], p_turned[:, e, :], ACT.Copy, scale=vs_col[:, t : t + 1])
-        turn_values(0)
-        nc.scalar.copy(vw0_bf[:, 1, :].rearrange("s (c i t) -> s c t i", i=4, t=PACK),
-                       w_planes[:].rearrange("s t (c i) -> s c t i", i=4))
+        def turn_weights(b, dst, bank):
+            w_turned = ps.tile([P, 2, P], F32, name=f"w_turned{b}", tag=bank)
+            for u in range(2):
+                w_pairs = sb.tile([P, P, 2], BF16, name=f"w_pairs{b}_{u}")
+                if b == 0:
+                    nc.gpsimd.tensor_tensor(w_pairs[:], vs_pairs[:, u, :, :], p[b][u][:], ALU.mult)
+                else:
+                    nc.vector.tensor_tensor(w_pairs[:], vs_wide[:, 2 * u : 2 * u + 2, :].rearrange("q e s -> q s e"),
+                                            p[b][u][:], ALU.mult)
+                nc.tensor.transpose(w_turned[:, u, :], w_pairs[:].rearrange("q s e -> q (s e)").bitcast(F32), ident[:])
+            nc.scalar.copy(dst.bitcast(F32).rearrange("s (q u) -> s q u", u=2), w_turned[:].rearrange("s u q -> s q u"))
 
-        w_turned = ps.tile([P, 2, P], F32, name="w_turned")
-        for u in range(2):
-            w_pairs = sb.tile([P, P, 2], BF16, name=f"w_pairs{u}")
-            nc.vector.tensor_tensor(w_pairs[:], vs_wide[:, 2 * u : 2 * u + 2, :].rearrange("q e s -> q s e"),
-                                    p1[u][:], ALU.mult)
-            nc.tensor.transpose(w_turned[:, u, :], w_pairs[:].rearrange("q s e -> q (s e)").bitcast(F32), ident[:])
-        nc.scalar.copy(w1_bf[:].bitcast(F32).rearrange("s (q u) -> s q u", u=2), w_turned[:].rearrange("s u q -> s q u"))
+        turn_values(0)
+        turn_weights(0, vw0_bf[:, 1, :], "bank0_0")
+        turn_weights(1, w1_bf[:], "bank0_1")
         turn_values(1)
 
         minus_one = sb.tile([P, QB], F32, name="minus_one")

@@ -119,29 +119,39 @@ def tile_attend_router_kernel(tc, xq, k_words, k_scales, vT, vs, offs, qoffs, ou
                 nc.tensor.matmul_mx(out=scores[b][j][:], lhsT=q_codes[:, cols].bitcast(FP8X4), lhsT_scale=q_bytes[:, cols],
                                     rhs=k_codes[:, slots].bitcast(FP8X4), rhs_scale=k_bytes[:, slots], start=True, stop=True)
 
-        neg_score = [sb.tile([P, 2, P, 2], F32, name=f"neg_score{b}") for b in range(QB)]
+        neg_score0 = sb.tile([P, 2, P // 2, 2], F32, name="neg_score0")
+        neg_score1 = sb.tile([P, 2, P, 2], F32, name="neg_score1")
         neg_max = [[sb.tile([P, 1], F32, name=f"neg_max{b}_{j}") for j in range(2)] for b in range(QB)]
-        for j in range(2):
-            s_half = slice(j * P // 2, (j + 1) * P // 2)
-            for b in range(QB):
-                dst = neg_score[b][:, :, s_half, :]
-                src = scores[b][j][:].rearrange("q (s u e) -> q u s e", u=2, e=2)
-                if j == 0:
-                    nc.vector.tensor_reduce(neg_max[b][0][:], scores[b][0][:], AX.X, ALU.max, negate=True)
-                    nc.scalar.activation(dst, src, ACT.Copy, scale=-1.0)
-                else:
-                    nc.vector.tensor_scalar(dst, src, -1.0, neg_max[b][0][:], ALU.mult, ALU.min, accum_out=neg_max[b][1][:])
-
+        halves = [slice(0, P // 2), slice(P // 2, P)]
+        by_pairs = [[scores[b][j][:].rearrange("q (s u e) -> q u s e", u=2, e=2) for j in range(2)] for b in range(QB)]
         sum_parts = sb.tile([P, 2, QB], F32, name="sum_parts")
-        p = [[sb.tile([P, P, 2], F32, name=f"p{b}_{u}") for u in range(2)] for b in range(QB)]
-        for b in range(QB):
-            for u in range(2):
-                nc.scalar.activation(p[b][u][:], neg_score[b][:, u, :, :], ACT.Exp, scale=-1.0,
-                                     bias=neg_max[b][1][:], accum_out=sum_parts[:, u, b : b + 1])
+        early = sb.tile([P, 2, P // 2, 2], F32, name="early")
+        early_vs = sb.tile([P, 2, P // 2, 2], F32, name="early_vs")
+        nc.vector.tensor_reduce(neg_max[0][0][:], scores[0][0][:], AX.X, ALU.max, negate=True)
+        nc.scalar.activation(early[:], by_pairs[0][0], ACT.Exp, bias=neg_max[0][0][:], accum_out=sum_parts[:, 0, 0:1])
+        nc.gpsimd.tensor_tensor(early_vs[:], vs_pairs[:, :, halves[0], :], early[:], ALU.mult)
+        nc.vector.tensor_reduce(neg_max[1][0][:], scores[1][0][:], AX.X, ALU.max, negate=True)
+        nc.scalar.activation(neg_score1[:, :, halves[0], :], by_pairs[1][0], ACT.Copy, scale=-1.0)
+        nc.vector.tensor_scalar(neg_score0[:], by_pairs[0][1], -1.0, neg_max[0][0][:], ALU.mult, ALU.min,
+                                accum_out=neg_max[0][1][:])
+        nc.vector.tensor_scalar(neg_score1[:, :, halves[1], :], by_pairs[1][1], -1.0, neg_max[1][0][:], ALU.mult, ALU.min,
+                                accum_out=neg_max[1][1][:])
+
+        late = sb.tile([P, 2, P // 2, 2], F32, name="late")
+        to_row_max = sb.tile([P, 1], F32, name="to_row_max")
+        nc.scalar.activation(late[:], neg_score0[:], ACT.Exp, scale=-1.0, bias=neg_max[0][1][:], accum_out=sum_parts[:, 1, 0:1])
+        nc.scalar.activation(to_row_max[:], neg_max[0][0][:], ACT.Exp, scale=-1.0, bias=neg_max[0][1][:])
+        p1 = [sb.tile([P, P, 2], F32, name=f"p1_{u}") for u in range(2)]
+        w0_pairs = sb.tile([P, 2, P, 2], BF16, name="w0_pairs")
+        nc.gpsimd.tensor_tensor(w0_pairs[:, :, halves[1], :], vs_pairs[:, :, halves[1], :], late[:], ALU.mult)
+        nc.scalar.activation(p1[0][:], neg_score1[:, 0, :, :], ACT.Exp, scale=-1.0,
+                             bias=neg_max[1][1][:], accum_out=sum_parts[:, 0, 1:2])
+        nc.scalar.activation(w0_pairs[:, :, halves[0], :], early_vs[:], ACT.Copy, scale=to_row_max[:])
+        nc.scalar.activation(p1[1][:], neg_score1[:, 1, :, :], ACT.Exp, scale=-1.0,
+                             bias=neg_max[1][1][:], accum_out=sum_parts[:, 1, 1:2])
         row_sum = sb.tile([P, QB], F32, name="row_sum")
-        for b in range(QB):
-            nc.scalar.activation(row_sum[:, b : b + 1], sum_parts[:, 0, b : b + 1], ACT.Identity,
-                                 bias=sum_parts[:, 1, b : b + 1])
+        nc.scalar.activation(row_sum[:, 0:1], sum_parts[:, 0, 0:1], ACT.Identity, scale=to_row_max[:], bias=sum_parts[:, 1, 0:1])
+        nc.scalar.activation(row_sum[:, 1:2], sum_parts[:, 0, 1:2], ACT.Identity, bias=sum_parts[:, 1, 1:2])
 
         vw0_bf = sb.tile([P, 2, N], BF16, name="vw0_bf", align_bytes=64)
         v1_bf = sb.tile([P, N], BF16, name="v1_bf", align_bytes=64)
@@ -174,21 +184,18 @@ def tile_attend_router_kernel(tc, xq, k_words, k_scales, vT, vs, offs, qoffs, ou
                                 rhs=codes[:, cols].bitcast(FP8X4), rhs_scale=scales[:, cols], start=True, stop=True)
             nc.scalar.copy(y_sb[h][:, first:last], y[:])
 
-        def turn_weights(b, dst, bank):
+        def turn_weights(b, pairs, dst, bank):
             w_turned = ps.tile([P, 2, P], F32, name=f"w_turned{b}", tag=bank)
             for u in range(2):
-                w_pairs = sb.tile([P, P, 2], BF16, name=f"w_pairs{b}_{u}")
-                if b == 0:
-                    nc.gpsimd.tensor_tensor(w_pairs[:], vs_pairs[:, u, :, :], p[b][u][:], ALU.mult)
-                else:
-                    nc.vector.tensor_tensor(w_pairs[:], vs_wide[:, 2 * u : 2 * u + 2, :].rearrange("q e s -> q s e"),
-                                            p[b][u][:], ALU.mult)
-                nc.tensor.transpose(w_turned[:, u, :], w_pairs[:].rearrange("q s e -> q (s e)").bitcast(F32), ident[:])
+                nc.tensor.transpose(w_turned[:, u, :], pairs[u].rearrange("q s e -> q (s e)").bitcast(F32), ident[:])
             nc.scalar.copy(dst.bitcast(F32).rearrange("s (q u) -> s q u", u=2), w_turned[:].rearrange("s u q -> s q u"))
 
+        turn_weights(0, [w0_pairs[:, u, :, :] for u in range(2)], vw0_bf[:, 1, :], "bank0_0")
         turn_values(0)
-        turn_weights(0, vw0_bf[:, 1, :], "bank0_0")
-        turn_weights(1, w1_bf[:], "bank0_1")
+        w1_pairs = [sb.tile([P, P, 2], BF16, name=f"w1_pairs{u}") for u in range(2)]
+        nc.gpsimd.tensor_tensor(w1_pairs[0][:], vs_pairs[:, 0, :, :], p1[0][:], ALU.mult)
+        nc.vector.tensor_tensor(w1_pairs[1][:], vs_wide[:, 2:4, :].rearrange("q e s -> q s e"), p1[1][:], ALU.mult)
+        turn_weights(1, [w1_pairs[u][:] for u in range(2)], w1_bf[:], "bank0_1")
         turn_values(1)
 
         minus_one = sb.tile([P, QB], F32, name="minus_one")

@@ -119,6 +119,12 @@ def tile_attend_router_kernel(tc, xq, k_words, k_scales, vT, vs, offs, qoffs, ou
                 nc.tensor.matmul_mx(out=scores[b][j][:], lhsT=q_codes[:, cols].bitcast(FP8X4), lhsT_scale=q_bytes[:, cols],
                                     rhs=k_codes[:, slots].bitcast(FP8X4), rhs_scale=k_bytes[:, slots], start=True, stop=True)
 
+        warm = ps.tile([P, HALF + P], F32, name="warm", tag="v_turned")
+        for first, last in ((0, HALF), (HALF, HALF + P)):
+            nc.tensor.matmul_mx(out=warm[:, first:last], lhsT=q_codes[:, P:NQ].bitcast(FP8X4), lhsT_scale=q_bytes[:, P:NQ],
+                                rhs=k_codes[:, N - (last - first) : N].bitcast(FP8X4), rhs_scale=k_bytes[:, N - (last - first) : N],
+                                start=True, stop=True)
+
         neg_score0 = sb.tile([P, 2, P // 2, 2], F32, name="neg_score0")
         neg_score1 = sb.tile([P, 2, P, 2], F32, name="neg_score1")
         neg_max = [[sb.tile([P, 1], F32, name=f"neg_max{b}_{j}") for j in range(2)] for b in range(QB)]
@@ -177,42 +183,40 @@ def tile_attend_router_kernel(tc, xq, k_words, k_scales, vT, vs, offs, qoffs, ou
         inv_wide = reused.tile([P, NQ], F32, name="inv_wide", align_bytes=64, offset=4 * 3 * P)
         y_sb = [sb.tile([P, NQ], F32, name=f"y_sb{h}") for h in range(EB)]
 
-        def product(h, first, last, bank):
+        def product(h, first, last, bank, copy):
             cols = slice(P + first, P + last)
             y = ps.tile([P, last - first], F32, name=f"y_{bank}", tag=bank)
             nc.tensor.matmul_mx(out=y[:], lhsT=v_codes[h].bitcast(FP8X4), lhsT_scale=v_scales[h],
                                 rhs=codes[:, cols].bitcast(FP8X4), rhs_scale=scales[:, cols], start=True, stop=True)
-            nc.scalar.copy(y_sb[h][:, first:last], y[:])
+            copy(y_sb[h][:, first:last], y[:])
 
-        def turn_weights(b, pairs, dst, bank):
+        def turn_weights(b, pairs, order, dst, bank):
             w_turned = ps.tile([P, 2, P], F32, name=f"w_turned{b}", tag=bank)
-            for u in range(2):
+            for u in order:
                 nc.tensor.transpose(w_turned[:, u, :], pairs[u].rearrange("q s e -> q (s e)").bitcast(F32), ident[:])
             nc.scalar.copy(dst.bitcast(F32).rearrange("s (q u) -> s q u", u=2), w_turned[:].rearrange("s u q -> s q u"))
 
-        turn_weights(0, [w0_pairs[:, u, :, :] for u in range(2)], vw0_bf[:, 1, :], "bank0_0")
+        turn_weights(0, [w0_pairs[:, u, :, :] for u in range(2)], (0, 1), vw0_bf[:, 1, :], "bank0_0")
         turn_values(0)
         w1_pairs = [sb.tile([P, P, 2], BF16, name=f"w1_pairs{u}") for u in range(2)]
         nc.gpsimd.tensor_tensor(w1_pairs[0][:], vs_pairs[:, 0, :, :], p1[0][:], ALU.mult)
         nc.vector.tensor_tensor(w1_pairs[1][:], vs_wide[:, 2:4, :].rearrange("q e s -> q s e"), p1[1][:], ALU.mult)
-        turn_weights(1, [w1_pairs[u][:] for u in range(2)], w1_bf[:], "bank0_1")
-        turn_values(1)
-
-        minus_one = sb.tile([P, QB], F32, name="minus_one")
-        nc.gpsimd.memset(minus_one[:], -1.0)
-        nc.gpsimd.tensor_tensor(inv_sum[:], row_sum[:], minus_one[:], ALU.pow)
-        inv_turned = ps.tile([P, QB, P], F32, name="inv_turned", tag="rows")
+        turn_weights(1, [w1_pairs[u][:] for u in range(2)], (1, 0), w1_bf[:], "bank0_1")
+        nc.vector.reciprocal(inv_sum[:], row_sum[:])
+        inv_turned = ps.tile([P, QB, P], F32, name="inv_turned", tag="bank1_1")
         for b in range(QB):
             nc.tensor.transpose(inv_turned[:, b, :], inv_sum[:, b : b + 1].to_broadcast([P, P]), ident[:])
+        turn_values(1)
+
 
         nc.vector.quantize_mx(out=codes[:, 0 : 2 * P].bitcast(FP8X4), scales=scales[:, 0 : 2 * P],
                               in_=vw0_bf[:].rearrange("s a n -> s (a n)"))
-        product(0, 0, P, "bank0_0")
+        product(0, 0, P, "bank0_0", nc.vector.tensor_copy)
         nc.vector.quantize_mx(out=codes[:, 2 * P : 3 * P].bitcast(FP8X4), scales=scales[:, 2 * P : 3 * P], in_=w1_bf[:])
-        product(0, P, NQ, "bank0_1")
-        nc.vector.tensor_copy(inv_wide[:], inv_turned[:].rearrange("f b q -> f (b q)"))
+        product(0, P, NQ, "bank0_1", nc.scalar.copy)
+        nc.scalar.copy(inv_wide[:], inv_turned[:].rearrange("f b q -> f (b q)"))
         nc.vector.quantize_mx(out=v1_codes[:].bitcast(FP8X4), scales=v1_scales[:], in_=v1_bf[:])
-        product(1, 0, NQ, "bank1_0")
+        product(1, 0, NQ, "bank1_0", nc.scalar.copy)
 
         for h in range(EB):
             nc.vector.tensor_tensor(result[h][:].indirect(query_list[:]), y_sb[h][:], inv_wide[:], ALU.mult)

@@ -119,12 +119,6 @@ def tile_attend_router_kernel(tc, xq, k_words, k_scales, vT, vs, offs, qoffs, ou
                 nc.tensor.matmul_mx(out=scores[b][j][:], lhsT=q_codes[:, cols].bitcast(FP8X4), lhsT_scale=q_bytes[:, cols],
                                     rhs=k_codes[:, slots].bitcast(FP8X4), rhs_scale=k_bytes[:, slots], start=True, stop=True)
 
-        warm = ps.tile([P, HALF + P], F32, name="warm", tag="v_turned")
-        for first, last in ((0, HALF), (HALF, HALF + P)):
-            nc.tensor.matmul_mx(out=warm[:, first:last], lhsT=q_codes[:, P:NQ].bitcast(FP8X4), lhsT_scale=q_bytes[:, P:NQ],
-                                rhs=k_codes[:, N - (last - first) : N].bitcast(FP8X4), rhs_scale=k_bytes[:, N - (last - first) : N],
-                                start=True, stop=True)
-
         neg_score0 = sb.tile([P, 2, P // 2, 2], F32, name="neg_score0")
         neg_score1 = sb.tile([P, 2, P, 2], F32, name="neg_score1")
         neg_max = [[sb.tile([P, 1], F32, name=f"neg_max{b}_{j}") for j in range(2)] for b in range(QB)]

@@ -32,11 +32,13 @@ def tile_attend_router_kernel(tc, xq, k_words, k_scales, vT, vs, offs, qoffs, ou
     with ExitStack() as ctx:
         sb = ctx.enter_context(tc.tile_pool(name="sb", bufs=1))
         reused = ctx.enter_context(tc.tile_pool(name="reused", bufs=1))
+        reused0 = ctx.enter_context(tc.tile_pool(name="reused0", bufs=1))
+        staged = ctx.enter_context(tc.tile_pool(name="staged", bufs=1))
         ps = ctx.enter_context(tc.psum_pool(name="ps", bufs=1))
 
         slot_list = sb.tile([P, N // 16], U16, name="slot_list")
         query_list = sb.tile([P, NQ // 16], U16, name="query_list")
-        xq_pool = [sb.tile([P, T], F32, name="xq_pool0", tag="xq0_then_v0"),
+        xq_pool = [reused0.tile([P, T], F32, name="xq_pool0", align_bytes=64, offset=0),
                    reused.tile([P, T], F32, name="xq_pool1", align_bytes=64, offset=0),
                    sb.tile([P, T], F32, name="xq_pool2"), sb.tile([P, T], F32, name="xq_pool3")]
         ks_pool = sb.tile([P, T], U8, name="ks_pool", tag="scales_then_words")
@@ -78,7 +80,7 @@ def tile_attend_router_kernel(tc, xq, k_words, k_scales, vT, vs, offs, qoffs, ou
         kw_pool = sb.tile([P, T], I32, name="kw_pool", tag="scales_then_words")
         nc.sync.dma_start(kw_pool[:], k_words[0].rearrange("s n t -> s (n t)").bitcast(I32))
         gather_queries(0)
-        v_pool = [sb.tile([P, T], F32, name="v_pool0", tag="xq0_then_v0")]
+        v_pool = [reused0.tile([P, T], F32, name="v_pool0", align_bytes=64, offset=0)]
         nc.sync.dma_start(v_pool[0][:], vT[0:P, :])
         gather_queries(1)
         v_pool.append(reused.tile([P, T], F32, name="v_pool1", align_bytes=64, offset=0))
@@ -124,11 +126,11 @@ def tile_attend_router_kernel(tc, xq, k_words, k_scales, vT, vs, offs, qoffs, ou
         neg_max = [[sb.tile([P, 1], F32, name=f"neg_max{b}_{j}") for j in range(2)] for b in range(QB)]
         halves = [slice(0, P // 2), slice(P // 2, P)]
         by_pairs = [[scores[b][j][:].rearrange("q (s u e) -> q u s e", u=2, e=2) for j in range(2)] for b in range(QB)]
-        sum_parts = sb.tile([P, 2, QB], F32, name="sum_parts")
+        sum_parts = sb.tile([P, 2], F32, name="sum_parts")
         early = sb.tile([P, 2, P // 2, 2], F32, name="early")
         early_vs = sb.tile([P, 2, P // 2, 2], F32, name="early_vs")
         nc.vector.tensor_reduce(neg_max[0][0][:], scores[0][0][:], AX.X, ALU.max, negate=True)
-        nc.scalar.activation(early[:], by_pairs[0][0], ACT.Exp, bias=neg_max[0][0][:], accum_out=sum_parts[:, 0, 0:1])
+        nc.scalar.activation(early[:], by_pairs[0][0], ACT.Exp, bias=neg_max[0][0][:], accum_out=sum_parts[:, 0:1])
         nc.gpsimd.tensor_tensor(early_vs[:], vs_pairs[:, :, halves[0], :], early[:], ALU.mult)
         nc.vector.tensor_reduce(neg_max[1][0][:], scores[1][0][:], AX.X, ALU.max, negate=True)
         nc.scalar.activation(neg_score1[:, :, halves[0], :], by_pairs[1][0], ACT.Copy, scale=-1.0)
@@ -139,42 +141,44 @@ def tile_attend_router_kernel(tc, xq, k_words, k_scales, vT, vs, offs, qoffs, ou
 
         late = sb.tile([P, 2, P // 2, 2], F32, name="late")
         to_row_max = sb.tile([P, 1], F32, name="to_row_max")
-        nc.scalar.activation(late[:], neg_score0[:], ACT.Exp, scale=-1.0, bias=neg_max[0][1][:], accum_out=sum_parts[:, 1, 0:1])
-        nc.scalar.activation(to_row_max[:], neg_max[0][0][:], ACT.Exp, scale=-1.0, bias=neg_max[0][1][:])
-        p1 = [sb.tile([P, P, 2], F32, name=f"p1_{u}") for u in range(2)]
-        w0_pairs = sb.tile([P, 2, P, 2], BF16, name="w0_pairs")
-        nc.gpsimd.tensor_tensor(w0_pairs[:, :, halves[1], :], vs_pairs[:, :, halves[1], :], late[:], ALU.mult)
-        nc.scalar.activation(p1[0][:], neg_score1[:, 0, :, :], ACT.Exp, scale=-1.0,
-                             bias=neg_max[1][1][:], accum_out=sum_parts[:, 0, 1:2])
-        nc.scalar.activation(w0_pairs[:, :, halves[0], :], early_vs[:], ACT.Copy, scale=to_row_max[:])
-        nc.scalar.activation(p1[1][:], neg_score1[:, 1, :, :], ACT.Exp, scale=-1.0,
-                             bias=neg_max[1][1][:], accum_out=sum_parts[:, 1, 1:2])
         row_sum = sb.tile([P, QB], F32, name="row_sum")
-        nc.scalar.activation(row_sum[:, 0:1], sum_parts[:, 0, 0:1], ACT.Identity, scale=to_row_max[:], bias=sum_parts[:, 1, 0:1])
-        nc.scalar.activation(row_sum[:, 1:2], sum_parts[:, 0, 1:2], ACT.Identity, bias=sum_parts[:, 1, 1:2])
+        p1 = sb.tile([P, 2, P, 2], F32, name="p1")
+        nc.scalar.activation(late[:], neg_score0[:], ACT.Exp, scale=-1.0, bias=neg_max[0][1][:], accum_out=sum_parts[:, 1:2])
+        nc.scalar.activation(to_row_max[:], neg_max[0][0][:], ACT.Exp, scale=-1.0, bias=neg_max[0][1][:])
+        nc.scalar.activation(row_sum[:, 0:1], sum_parts[:, 0:1], ACT.Identity, scale=to_row_max[:], bias=sum_parts[:, 1:2])
+        w0_pairs = sb.tile([P, 2, P, 2], BF16, name="w0_pairs")
+        w1_first = sb.tile([P, P, 2], BF16, name="w1_first")
+        nc.gpsimd.tensor_tensor(w0_pairs[:, :, halves[1], :], vs_pairs[:, :, halves[1], :], late[:], ALU.mult)
+        nc.scalar.activation(w0_pairs[:, :, halves[0], :], early_vs[:], ACT.Copy, scale=to_row_max[:])
+        nc.scalar.activation(p1[:], neg_score1[:], ACT.Exp, scale=-1.0, bias=neg_max[1][1][:], accum_out=row_sum[:, 1:2])
+        nc.gpsimd.tensor_tensor(w1_first[:], vs_pairs[:, 0, :, :], p1[:, 0, :, :], ALU.mult)
 
         vw0_bf = sb.tile([P, 2, N], BF16, name="vw0_bf", align_bytes=64)
         v1_bf = sb.tile([P, N], BF16, name="v1_bf", align_bytes=64)
         w1_bf = sb.tile([P, N], BF16, name="w1_bf", align_bytes=64)
-        codes = reused.tile([P, 3 * P], U32, name="codes", align_bytes=64, offset=0)
         scales = sb.tile([P, 3 * P], U8, name="scales", align_bytes=64)
         v1_codes = sb.tile([P, P], U32, name="v1_codes", align_bytes=64)
         v1_scales = sb.tile([P, P], U8, name="v1_scales", align_bytes=64)
         v_bf = [vw0_bf[:, 0, :], v1_bf[:]]
-        v_codes = [codes[:, 0:P], v1_codes[:]]
         v_scales = [scales[:, 0:P], v1_scales[:]]
 
         def turn_values(h):
             picked = sb.tile([P, 2, P, 2], BF16, name=f"v_picked{h}")
-            nc.vector.tensor_copy(picked[:].rearrange("f u s e -> f s u e"), v_pool[h][:].indirect(slot_list[:]))
             pairs = picked[:].rearrange("f u s e -> f (u s e)").bitcast(F32)
+            if h == 0:
+                nc.vector.tensor_copy(picked[:].rearrange("f u s e -> f s u e"), v_pool[h][:].indirect(slot_list[:]))
+            else:
+                stage = staged.tile([P, HALF], BF16, name="stage", align_bytes=64, offset=4 * (2 * P - P // 2))
+                nc.vector.tensor_copy(stage[:], v_pool[h][:].indirect(slot_list[:, 0 : HALF // 16]))
+                nc.gpsimd.tensor_copy(picked[:, :, halves[0], :], stage[:].rearrange("f (s u e) -> f u s e", u=2, e=2))
+                nc.vector.tensor_copy(picked[:, :, halves[1], :].rearrange("f u s e -> f s u e"),
+                                      v_pool[h][:].indirect(slot_list[:, HALF // 16 : N // 16]))
             v_turned = ps.tile([P, 2, P], F32, name=f"v_turned{h}", tag="v_turned")
             for u in range(2):
                 nc.tensor.transpose(v_turned[:, u, :], pairs[:, u * P : (u + 1) * P], ident[:])
             nc.scalar.copy(v_bf[h].bitcast(F32).rearrange("s (f u) -> s f u", u=2), v_turned[:].rearrange("s u f -> s f u"))
 
-        inv_sum = sb.tile([P, QB], F32, name="inv_sum")
-        inv_wide = reused.tile([P, NQ], F32, name="inv_wide", align_bytes=64, offset=4 * 3 * P)
+        inv_wide = reused.tile([P, NQ], F32, name="inv_wide", align_bytes=64, offset=0)
         y_sb = [sb.tile([P, NQ], F32, name=f"y_sb{h}") for h in range(EB)]
 
         def product(h, first, last, bank, copy):
@@ -192,16 +196,17 @@ def tile_attend_router_kernel(tc, xq, k_words, k_scales, vT, vs, offs, qoffs, ou
 
         turn_weights(0, [w0_pairs[:, u, :, :] for u in range(2)], (0, 1), vw0_bf[:, 1, :], "bank0_0")
         turn_values(0)
-        w1_pairs = [sb.tile([P, P, 2], BF16, name=f"w1_pairs{u}") for u in range(2)]
-        nc.gpsimd.tensor_tensor(w1_pairs[0][:], vs_pairs[:, 0, :, :], p1[0][:], ALU.mult)
-        nc.vector.tensor_tensor(w1_pairs[1][:], vs_wide[:, 2:4, :].rearrange("q e s -> q s e"), p1[1][:], ALU.mult)
-        turn_weights(1, [w1_pairs[u][:] for u in range(2)], (1, 0), w1_bf[:], "bank0_1")
+        w1_second = sb.tile([P, P, 2], BF16, name="w1_second")
+        nc.vector.tensor_tensor(w1_second[:], vs_wide[:, 2:4, :].rearrange("q e s -> q s e"), p1[:, 1, :, :], ALU.mult)
+        turn_weights(1, [w1_first[:], w1_second[:]], (1, 0), w1_bf[:], "bank0_1")
+        inv_sum = sb.tile([P, QB], F32, name="inv_sum")
         nc.vector.reciprocal(inv_sum[:], row_sum[:])
         inv_turned = ps.tile([P, QB, P], F32, name="inv_turned", tag="bank1_1")
         for b in range(QB):
             nc.tensor.transpose(inv_turned[:, b, :], inv_sum[:, b : b + 1].to_broadcast([P, P]), ident[:])
         turn_values(1)
-
+        codes = staged.tile([P, 3 * P], U32, name="codes", align_bytes=64, offset=0)
+        v_codes = [codes[:, 0:P], v1_codes[:]]
 
         nc.vector.quantize_mx(out=codes[:, 0 : 2 * P].bitcast(FP8X4), scales=scales[:, 0 : 2 * P],
                               in_=vw0_bf[:].rearrange("s a n -> s (a n)"))

@@ -21,7 +21,8 @@ QB = NQ // P
 EB = DV // P
 HALF = N // 2
 SCALE_STEP = P // (D // 32)
-VS_ROW = 4
+VS_RUN = T // P
+BANK = 512
 
 FLOPS = 2 * NQ * N * (D + DV)
 BYTES = 4 * D * T + D * T + (D // 32) * T + 4 * DV * T + 4 * T + 2 * P * (N + NQ) // 16 + 4 * DV * T
@@ -45,8 +46,9 @@ def tile_attend_router_kernel(tc, xq, k_words, k_scales, vT, vs, offs, qoffs, ou
         vs_pool = sb.tile([P, T], F32, name="vs_pool")
         result = [sb.tile([P, T], F32, name=f"result{h}") for h in range(EB)]
 
-        nc.gpsimd.memset(ks_pool[:].bitcast(I32), 0)
-        nc.vector.memset(vs_pool[:], 0.0)
+        nc.vector.memset(ks_pool[:].bitcast(I32), 0)
+        vs_cols = sb.tile([P, VS_RUN], F32, name="vs_cols")
+        nc.scalar.dma_start(vs_cols[:], vs[0, :].rearrange("(p j) -> p j", j=VS_RUN))
 
         xq_planes = xq.rearrange("(s t) n -> s t n", t=PACK)
         nc.sync.dma_start(xq_pool[0][:], xq_planes[:, 0, :])
@@ -54,12 +56,18 @@ def tile_attend_router_kernel(tc, xq, k_words, k_scales, vT, vs, offs, qoffs, ou
         nc.sync.dma_start(ks_pool[0:P:SCALE_STEP, :].bitcast(I32), k_scales[0].bitcast(I32))
         nc.sync.dma_start(query_list[:], qoffs)
         nc.sync.dma_start(xq_pool[1][:], xq_planes[:, 1, :])
-        nc.sync.dma_start(vs_pool[VS_ROW : VS_ROW + 1, :], vs[0:1, :])
         nc.sync.dma_start(xq_pool[2][:], xq_planes[:, 2, :])
         nc.sync.dma_start(xq_pool[3][:], xq_planes[:, 3, :])
 
         ident = sb.tile([P, P], F32, name="ident")
         make_identity(nc, ident[:])
+        vs_tokens = vs_pool[:].rearrange("r (p j) -> r p j", j=VS_RUN)
+        for a in range(T // BANK):
+            spread = ps.tile([P, BANK // P, P], F32, name=f"vs_spread{a}", tag=f"bank{a // 2}_{a % 2}")
+            for j in range(BANK // P):
+                column = a * (BANK // P) + j
+                nc.tensor.transpose(spread[:, j, :], vs_cols[:, column : column + 1].to_broadcast([P, P]), ident[:])
+            nc.scalar.copy(vs_tokens[:, :, a * (BANK // P) : (a + 1) * (BANK // P)], spread[:].rearrange("r j p -> r p j"))
         for h in range(EB):
             nc.gpsimd.memset(result[h][:], 0.0)
 
@@ -86,18 +94,17 @@ def tile_attend_router_kernel(tc, xq, k_words, k_scales, vT, vs, offs, qoffs, ou
         v_pool.append(reused.tile([P, T], F32, name="v_pool1", align_bytes=64, offset=0))
         nc.sync.dma_start(v_pool[1][:], vT[P : 2 * P, :])
 
-        nc.vector.tensor_copy(vs_row[:], vs_pool[:].indirect(slot_list[:]))
-        vs_turned = ps.tile([P, PACK, P], F32, name="vs_turned", tag="rows")
-        for t in range(PACK):
-            nc.tensor.transpose(vs_turned[:, t, :], vs_row[:, t:N:PACK], ident[:])
-        vs_col = sb.tile([P, PACK], F32, name="vs_col")
-        nc.scalar.copy(vs_col[:], vs_turned[:, :, VS_ROW])
-        vs_wide = ps.tile([P, PACK, P], F32, name="vs_wide", tag="rows")
-        for t in range(PACK):
-            nc.tensor.transpose(vs_wide[:, t, :], vs_col[:, t : t + 1].to_broadcast([P, P]), ident[:])
-
+        nc.scalar.activation(vs_row[:], vs_pool[:].indirect(slot_list[:]), ACT.Copy)
         vs_pairs = sb.tile([P, 2, P, 2], F32, name="vs_pairs")
-        nc.scalar.copy(vs_pairs[:], vs_wide[:].rearrange("q (u e) s -> q u s e", e=2))
+        nc.scalar.copy(vs_pairs[:], vs_row[:].rearrange("q (s u e) -> q u s e", u=2, e=2))
+        vs_back = ps.tile([P, 2, P], F32, name="vs_back", tag="bank0_0")
+        for e in range(2):
+            nc.tensor.transpose(vs_back[:, e, :], vs_row[:, 2 + e : N : PACK], ident[:])
+        vs_col = sb.tile([P, 2], F32, name="vs_col")
+        nc.scalar.copy(vs_col[:], vs_back[:, :, 0])
+        vs_wide = ps.tile([P, 2, P], F32, name="vs_wide", tag="rows")
+        for e in range(2):
+            nc.tensor.transpose(vs_wide[:, e, :], vs_col[:, e : e + 1].to_broadcast([P, P]), ident[:])
 
         gather_queries(2)
         gather_queries(3)
@@ -197,7 +204,7 @@ def tile_attend_router_kernel(tc, xq, k_words, k_scales, vT, vs, offs, qoffs, ou
         turn_weights(0, [w0_pairs[:, u, :, :] for u in range(2)], (0, 1), vw0_bf[:, 1, :], "bank0_0")
         turn_values(0)
         w1_second = sb.tile([P, P, 2], BF16, name="w1_second")
-        nc.vector.tensor_tensor(w1_second[:], vs_wide[:, 2:4, :].rearrange("q e s -> q s e"), p1[:, 1, :, :], ALU.mult)
+        nc.vector.tensor_tensor(w1_second[:], vs_wide[:].rearrange("q e s -> q s e"), p1[:, 1, :, :], ALU.mult)
         turn_weights(1, [w1_first[:], w1_second[:]], (1, 0), w1_bf[:], "bank0_1")
         inv_sum = sb.tile([P, QB], F32, name="inv_sum")
         nc.vector.reciprocal(inv_sum[:], row_sum[:])

@@ -46,7 +46,7 @@ def tile_attend_router_kernel(tc, xq, k_words, k_scales, vT, vs, offs, qoffs, ou
         vs_pool = sb.tile([P, T], F32, name="vs_pool")
         result = [sb.tile([P, T], F32, name=f"result{h}") for h in range(EB)]
 
-        nc.vector.memset(ks_pool[:].bitcast(I32), 0)
+        nc.gpsimd.memset(ks_pool[:].bitcast(I32), 0)
         vs_cols = sb.tile([P, VS_RUN], F32, name="vs_cols")
         nc.scalar.dma_start(vs_cols[:], vs[0, :].rearrange("(p j) -> p j", j=VS_RUN))
 

@@ -21,8 +21,9 @@ QB = NQ // P
 EB = DV // P
 HALF = N // 2
 SCALE_STEP = P // (D // 32)
-VS_RUN = T // P
-BANK = 512
+VS_ROW = 4
+
+SPLIT = 320
 
 FLOPS = 2 * NQ * N * (D + DV)
 BYTES = 4 * D * T + D * T + (D // 32) * T + 4 * DV * T + 4 * T + 2 * P * (N + NQ) // 16 + 4 * DV * T
@@ -35,6 +36,8 @@ def tile_attend_router_kernel(tc, xq, k_words, k_scales, vT, vs, offs, qoffs, ou
         reused = ctx.enter_context(tc.tile_pool(name="reused", bufs=1))
         reused0 = ctx.enter_context(tc.tile_pool(name="reused0", bufs=1))
         staged = ctx.enter_context(tc.tile_pool(name="staged", bufs=1))
+        after_q = ctx.enter_context(tc.tile_pool(name="after_q", bufs=1))
+        after_sums = ctx.enter_context(tc.tile_pool(name="after_sums", bufs=1))
         ps = ctx.enter_context(tc.psum_pool(name="ps", bufs=1))
 
         slot_list = sb.tile([P, N // 16], U16, name="slot_list")
@@ -47,8 +50,7 @@ def tile_attend_router_kernel(tc, xq, k_words, k_scales, vT, vs, offs, qoffs, ou
         result = [sb.tile([P, T], F32, name=f"result{h}") for h in range(EB)]
 
         nc.gpsimd.memset(ks_pool[:].bitcast(I32), 0)
-        vs_cols = sb.tile([P, VS_RUN], F32, name="vs_cols")
-        nc.scalar.dma_start(vs_cols[:], vs[0, :].rearrange("(p j) -> p j", j=VS_RUN))
+        nc.vector.memset(vs_pool[:], 0.0)
 
         xq_planes = xq.rearrange("(s t) n -> s t n", t=PACK)
         nc.sync.dma_start(xq_pool[0][:], xq_planes[:, 0, :])
@@ -56,22 +58,16 @@ def tile_attend_router_kernel(tc, xq, k_words, k_scales, vT, vs, offs, qoffs, ou
         nc.sync.dma_start(ks_pool[0:P:SCALE_STEP, :].bitcast(I32), k_scales[0].bitcast(I32))
         nc.sync.dma_start(query_list[:], qoffs)
         nc.sync.dma_start(xq_pool[1][:], xq_planes[:, 1, :])
+        nc.sync.dma_start(vs_pool[VS_ROW : VS_ROW + 1, :], vs[0:1, :])
         nc.sync.dma_start(xq_pool[2][:], xq_planes[:, 2, :])
         nc.sync.dma_start(xq_pool[3][:], xq_planes[:, 3, :])
 
         ident = sb.tile([P, P], F32, name="ident")
         make_identity(nc, ident[:])
-        vs_tokens = vs_pool[:].rearrange("r (p j) -> r p j", j=VS_RUN)
-        for a in range(T // BANK):
-            spread = ps.tile([P, BANK // P, P], F32, name=f"vs_spread{a}", tag=f"bank{a // 2}_{a % 2}")
-            for j in range(BANK // P):
-                column = a * (BANK // P) + j
-                nc.tensor.transpose(spread[:, j, :], vs_cols[:, column : column + 1].to_broadcast([P, P]), ident[:])
-            nc.scalar.copy(vs_tokens[:, :, a * (BANK // P) : (a + 1) * (BANK // P)], spread[:].rearrange("r j p -> r p j"))
         for h in range(EB):
             nc.gpsimd.memset(result[h][:], 0.0)
 
-        q_bf = sb.tile([P, NQ, PACK], BF16, name="q_bf", align_bytes=64)
+        q_bf = after_q.tile([P, NQ, PACK], BF16, name="q_bf", align_bytes=64, offset=0)
 
         def gather_queries(t):
             nc.vector.tensor_copy(q_bf[:, :, t], xq_pool[t][:].indirect(query_list[:]))
@@ -94,17 +90,16 @@ def tile_attend_router_kernel(tc, xq, k_words, k_scales, vT, vs, offs, qoffs, ou
         v_pool.append(reused.tile([P, T], F32, name="v_pool1", align_bytes=64, offset=0))
         nc.sync.dma_start(v_pool[1][:], vT[P : 2 * P, :])
 
-        nc.scalar.activation(vs_row[:], vs_pool[:].indirect(slot_list[:]), ACT.Copy)
-        vs_pairs = sb.tile([P, 2, P, 2], F32, name="vs_pairs")
-        nc.scalar.copy(vs_pairs[:], vs_row[:].rearrange("q (s u e) -> q u s e", u=2, e=2))
-        vs_back = ps.tile([P, 2, P], F32, name="vs_back", tag="bank0_0")
-        for e in range(2):
-            nc.tensor.transpose(vs_back[:, e, :], vs_row[:, 2 + e : N : PACK], ident[:])
-        vs_col = sb.tile([P, 2], F32, name="vs_col")
-        nc.scalar.copy(vs_col[:], vs_back[:, :, 0])
-        vs_wide = ps.tile([P, 2, P], F32, name="vs_wide", tag="rows")
-        for e in range(2):
-            nc.tensor.transpose(vs_wide[:, e, :], vs_col[:, e : e + 1].to_broadcast([P, P]), ident[:])
+        nc.vector.tensor_copy(vs_row[:].rearrange("q (u s e) -> q s u e", u=2, e=2), vs_pool[:].indirect(slot_list[:]))
+        vs_turned = ps.tile([P, PACK, P], F32, name="vs_turned", tag="rows")
+        for a in range(PACK):
+            nc.tensor.transpose(vs_turned[:, a, :], vs_row[:, a * P : (a + 1) * P], ident[:])
+        vs_col = sb.tile([P, PACK], F32, name="vs_col")
+        nc.vector.tensor_copy(vs_col[:], vs_turned[:, :, VS_ROW])
+        vs_wide = ps.tile([P, PACK, P], F32, name="vs_wide", tag="rows")
+        for a in range(PACK):
+            nc.tensor.transpose(vs_wide[:, a, :], vs_col[:, a : a + 1].to_broadcast([P, P]), ident[:])
+        vs_pairs = vs_wide[:].rearrange("q (u h) (s e) -> q u (h s) e", u=2, e=2)
 
         gather_queries(2)
         gather_queries(3)
@@ -117,6 +112,9 @@ def tile_attend_router_kernel(tc, xq, k_words, k_scales, vT, vs, offs, qoffs, ou
             nc.vector.quantize_mx(out=q_codes[:, cols].bitcast(FP8X4), scales=q_bytes[:, cols],
                                   in_=q_flat[:, b * P * PACK : (b + 1) * P * PACK])
 
+        vs_late = after_q.tile([P, 2, P // 2, 2], F32, name="vs_late", align_bytes=64, offset=0)
+        nc.vector.tensor_copy(vs_late[:], vs_pairs[:, :, P // 2 : P, :])
+
         scores = [[ps.tile([P, HALF], F32, name=f"score{b}_{j}", tag=f"bank{b}_{j}") for j in range(2)]
                   for b in range(QB)]
         for j in range(2):
@@ -128,39 +126,43 @@ def tile_attend_router_kernel(tc, xq, k_words, k_scales, vT, vs, offs, qoffs, ou
                 nc.tensor.matmul_mx(out=scores[b][j][:], lhsT=q_codes[:, cols].bitcast(FP8X4), lhsT_scale=q_bytes[:, cols],
                                     rhs=k_codes[:, slots].bitcast(FP8X4), rhs_scale=k_bytes[:, slots], start=True, stop=True)
 
-        neg_score0 = sb.tile([P, 2, P // 2, 2], F32, name="neg_score0")
-        neg_score1 = sb.tile([P, 2, P, 2], F32, name="neg_score1")
-        neg_max = [[sb.tile([P, 1], F32, name=f"neg_max{b}_{j}") for j in range(2)] for b in range(QB)]
         halves = [slice(0, P // 2), slice(P // 2, P)]
         by_pairs = [[scores[b][j][:].rearrange("q (s u e) -> q u s e", u=2, e=2) for j in range(2)] for b in range(QB)]
-        sum_parts = sb.tile([P, 2], F32, name="sum_parts")
-        early = sb.tile([P, 2, P // 2, 2], F32, name="early")
-        early_vs = sb.tile([P, 2, P // 2, 2], F32, name="early_vs")
+        neg_max = [[sb.tile([P, 1], F32, name=f"neg_max{b}_{j}") for j in range(2)] for b in range(QB)]
+        neg_score = [sb.tile([P, 2, P // 2, 2], F32, name=f"neg_score{b}") for b in range(QB)]
+        p = [[sb.tile([P, 2, P // 2, 2], F32, name=f"p{b}_{j}") for j in range(2)] for b in range(QB)]
+        sum_parts = [sb.tile([P, 2], F32, name="sum_parts0"),
+                     after_sums.tile([P, 2], F32, name="sum_parts1", align_bytes=64, offset=0)]
         nc.vector.tensor_reduce(neg_max[0][0][:], scores[0][0][:], AX.X, ALU.max, negate=True)
-        nc.scalar.activation(early[:], by_pairs[0][0], ACT.Exp, bias=neg_max[0][0][:], accum_out=sum_parts[:, 0:1])
-        nc.gpsimd.tensor_tensor(early_vs[:], vs_pairs[:, :, halves[0], :], early[:], ALU.mult)
+        nc.scalar.activation(p[0][0][:], by_pairs[0][0], ACT.Exp, bias=neg_max[0][0][:], accum_out=sum_parts[0][:, 0:1])
         nc.vector.tensor_reduce(neg_max[1][0][:], scores[1][0][:], AX.X, ALU.max, negate=True)
-        nc.scalar.activation(neg_score1[:, :, halves[0], :], by_pairs[1][0], ACT.Copy, scale=-1.0)
-        nc.vector.tensor_scalar(neg_score0[:], by_pairs[0][1], -1.0, neg_max[0][0][:], ALU.mult, ALU.min,
-                                accum_out=neg_max[0][1][:])
-        nc.vector.tensor_scalar(neg_score1[:, :, halves[1], :], by_pairs[1][1], -1.0, neg_max[1][0][:], ALU.mult, ALU.min,
-                                accum_out=neg_max[1][1][:])
+        for b in range(QB):
+            nc.vector.tensor_scalar(neg_score[b][:], by_pairs[b][1], -1.0, neg_max[b][0][:], ALU.mult, ALU.min,
+                                    accum_out=neg_max[b][1][:])
 
-        late = sb.tile([P, 2, P // 2, 2], F32, name="late")
+        picked = [sb.tile([P, N], BF16, name=f"v_picked{h}") for h in range(EB)]
+        nc.scalar.activation(picked[0][:, SPLIT:N], v_pool[0][:].indirect(slot_list[:, SPLIT // 16 : N // 16]), ACT.Copy)
+        nc.vector.tensor_copy(picked[0][:, 0:SPLIT], v_pool[0][:].indirect(slot_list[:, 0 : SPLIT // 16]))
+
         to_row_max = sb.tile([P, 1], F32, name="to_row_max")
         row_sum = sb.tile([P, QB], F32, name="row_sum")
-        p1 = sb.tile([P, 2, P, 2], F32, name="p1")
-        nc.scalar.activation(late[:], neg_score0[:], ACT.Exp, scale=-1.0, bias=neg_max[0][1][:], accum_out=sum_parts[:, 1:2])
+        w_pairs = [sb.tile([P, 2, P, 2], BF16, name=f"w_pairs{b}") for b in range(QB)]
         nc.scalar.activation(to_row_max[:], neg_max[0][0][:], ACT.Exp, scale=-1.0, bias=neg_max[0][1][:])
-        nc.scalar.activation(row_sum[:, 0:1], sum_parts[:, 0:1], ACT.Identity, scale=to_row_max[:], bias=sum_parts[:, 1:2])
-        w0_pairs = sb.tile([P, 2, P, 2], BF16, name="w0_pairs")
-        w1_first = sb.tile([P, P, 2], BF16, name="w1_first")
-        nc.gpsimd.tensor_tensor(w0_pairs[:, :, halves[1], :], vs_pairs[:, :, halves[1], :], late[:], ALU.mult)
-        nc.scalar.activation(w0_pairs[:, :, halves[0], :], early_vs[:], ACT.Copy, scale=to_row_max[:])
-        nc.scalar.activation(p1[:], neg_score1[:], ACT.Exp, scale=-1.0, bias=neg_max[1][1][:], accum_out=row_sum[:, 1:2])
-        nc.gpsimd.tensor_tensor(w1_first[:], vs_pairs[:, 0, :, :], p1[:, 0, :, :], ALU.mult)
+        nc.scalar.activation(p[0][1][:], neg_score[0][:], ACT.Exp, scale=-1.0, bias=neg_max[0][1][:], accum_out=sum_parts[0][:, 1:2])
+        nc.scalar.activation(p[1][0][:], by_pairs[1][0], ACT.Exp, bias=neg_max[1][1][:], accum_out=sum_parts[1][:, 0:1])
+        nc.scalar.activation(p[1][1][:], neg_score[1][:], ACT.Exp, scale=-1.0, bias=neg_max[1][1][:], accum_out=sum_parts[1][:, 1:2])
+        nc.scalar.activation(row_sum[:, 0:1], sum_parts[0][:, 0:1], ACT.Identity, scale=to_row_max[:], bias=sum_parts[0][:, 1:2])
+        nc.scalar.activation(row_sum[:, 1:2], sum_parts[1][:, 0:1], ACT.Identity, bias=sum_parts[1][:, 1:2])
+        flat = "q u s e -> q u (s e)"
+        nc.vector.scalar_tensor_tensor(w_pairs[0][:, :, halves[0], :].rearrange(flat), p[0][0][:].rearrange(flat), to_row_max[:],
+                                       vs_pairs[:, :, halves[0], :].rearrange(flat), ALU.mult, ALU.mult)
+        nc.gpsimd.tensor_tensor(w_pairs[0][:, :, halves[1], :], p[0][1][:], vs_late[:], ALU.mult)
+        for j in range(2):
+            nc.vector.tensor_tensor(w_pairs[1][:, :, halves[j], :], p[1][j][:], vs_pairs[:, :, halves[j], :], ALU.mult)
+        inv_sum = sb.tile([P, QB], F32, name="inv_sum")
+        nc.vector.reciprocal(inv_sum[:], row_sum[:])
 
-        vw0_bf = sb.tile([P, 2, N], BF16, name="vw0_bf", align_bytes=64)
+        vw0_bf = after_sums.tile([P, 2, N], BF16, name="vw0_bf", align_bytes=64, offset=0)
         v1_bf = sb.tile([P, N], BF16, name="v1_bf", align_bytes=64)
         w1_bf = sb.tile([P, N], BF16, name="w1_bf", align_bytes=64)
         scales = sb.tile([P, 3 * P], U8, name="scales", align_bytes=64)
@@ -170,22 +172,13 @@ def tile_attend_router_kernel(tc, xq, k_words, k_scales, vT, vs, offs, qoffs, ou
         v_scales = [scales[:, 0:P], v1_scales[:]]
 
         def turn_values(h):
-            picked = sb.tile([P, 2, P, 2], BF16, name=f"v_picked{h}")
-            pairs = picked[:].rearrange("f u s e -> f (u s e)").bitcast(F32)
-            if h == 0:
-                nc.vector.tensor_copy(picked[:].rearrange("f u s e -> f s u e"), v_pool[h][:].indirect(slot_list[:]))
-            else:
-                stage = staged.tile([P, HALF], BF16, name="stage", align_bytes=64, offset=4 * (2 * P - P // 2))
-                nc.vector.tensor_copy(stage[:], v_pool[h][:].indirect(slot_list[:, 0 : HALF // 16]))
-                nc.gpsimd.tensor_copy(picked[:, :, halves[0], :], stage[:].rearrange("f (s u e) -> f u s e", u=2, e=2))
-                nc.vector.tensor_copy(picked[:, :, halves[1], :].rearrange("f u s e -> f s u e"),
-                                      v_pool[h][:].indirect(slot_list[:, HALF // 16 : N // 16]))
+            pairs = picked[h][:].bitcast(F32)
             v_turned = ps.tile([P, 2, P], F32, name=f"v_turned{h}", tag="v_turned")
             for u in range(2):
-                nc.tensor.transpose(v_turned[:, u, :], pairs[:, u * P : (u + 1) * P], ident[:])
+                nc.tensor.transpose(v_turned[:, u, :], pairs[:, u : N // 2 : 2], ident[:])
             nc.scalar.copy(v_bf[h].bitcast(F32).rearrange("s (f u) -> s f u", u=2), v_turned[:].rearrange("s u f -> s f u"))
 
-        inv_wide = reused.tile([P, NQ], F32, name="inv_wide", align_bytes=64, offset=0)
+        inv_wide = sb.tile([P, NQ], F32, name="inv_wide")
         y_sb = [sb.tile([P, NQ], F32, name=f"y_sb{h}") for h in range(EB)]
 
         def product(h, first, last, bank, copy):
@@ -201,16 +194,16 @@ def tile_attend_router_kernel(tc, xq, k_words, k_scales, vT, vs, offs, qoffs, ou
                 nc.tensor.transpose(w_turned[:, u, :], pairs[u].rearrange("q s e -> q (s e)").bitcast(F32), ident[:])
             nc.scalar.copy(dst.bitcast(F32).rearrange("s (q u) -> s q u", u=2), w_turned[:].rearrange("s u q -> s q u"))
 
-        turn_weights(0, [w0_pairs[:, u, :, :] for u in range(2)], (0, 1), vw0_bf[:, 1, :], "bank0_0")
         turn_values(0)
-        w1_second = sb.tile([P, P, 2], BF16, name="w1_second")
-        nc.vector.tensor_tensor(w1_second[:], vs_wide[:].rearrange("q e s -> q s e"), p1[:, 1, :, :], ALU.mult)
-        turn_weights(1, [w1_first[:], w1_second[:]], (1, 0), w1_bf[:], "bank0_1")
-        inv_sum = sb.tile([P, QB], F32, name="inv_sum")
-        nc.vector.reciprocal(inv_sum[:], row_sum[:])
+        turn_weights(0, [w_pairs[0][:, u, :, :] for u in range(2)], (0, 1), vw0_bf[:, 1, :], "bank0_0")
+        turn_weights(1, [w_pairs[1][:, u, :, :] for u in range(2)], (0, 1), w1_bf[:], "bank0_1")
         inv_turned = ps.tile([P, QB, P], F32, name="inv_turned", tag="bank1_1")
         for b in range(QB):
             nc.tensor.transpose(inv_turned[:, b, :], inv_sum[:, b : b + 1].to_broadcast([P, P]), ident[:])
+        stage = staged.tile([P, HALF], BF16, name="stage", align_bytes=64, offset=4 * (2 * P - P // 2))
+        nc.vector.tensor_copy(stage[:], v_pool[1][:].indirect(slot_list[:, 0 : HALF // 16]))
+        nc.gpsimd.tensor_copy(picked[1][:, 0:HALF], stage[:])
+        nc.vector.tensor_copy(picked[1][:, HALF:N], v_pool[1][:].indirect(slot_list[:, HALF // 16 : N // 16]))
         turn_values(1)
         codes = staged.tile([P, 3 * P], U32, name="codes", align_bytes=64, offset=0)
         v_codes = [codes[:, 0:P], v1_codes[:]]

@@ -24,6 +24,7 @@ SCALE_STEP = P // (D // 32)
 VS_ROW = 4
 
 SPLIT = 320
+SPLIT1 = 384
 
 FLOPS = 2 * NQ * N * (D + DV)
 BYTES = 4 * D * T + D * T + (D // 32) * T + 4 * DV * T + 4 * T + 2 * P * (N + NQ) // 16 + 4 * DV * T
@@ -35,7 +36,6 @@ def tile_attend_router_kernel(tc, xq, k_words, k_scales, vT, vs, offs, qoffs, ou
         sb = ctx.enter_context(tc.tile_pool(name="sb", bufs=1))
         reused = ctx.enter_context(tc.tile_pool(name="reused", bufs=1))
         reused0 = ctx.enter_context(tc.tile_pool(name="reused0", bufs=1))
-        staged = ctx.enter_context(tc.tile_pool(name="staged", bufs=1))
         after_q = ctx.enter_context(tc.tile_pool(name="after_q", bufs=1))
         after_sums = ctx.enter_context(tc.tile_pool(name="after_sums", bufs=1))
         ps = ctx.enter_context(tc.psum_pool(name="ps", bufs=1))
@@ -188,24 +188,22 @@ def tile_attend_router_kernel(tc, xq, k_words, k_scales, vT, vs, offs, qoffs, ou
                                 rhs=codes[:, cols].bitcast(FP8X4), rhs_scale=scales[:, cols], start=True, stop=True)
             copy(y_sb[h][:, first:last], y[:])
 
-        def turn_weights(b, pairs, order, dst, bank):
+        def turn_weights(b, pairs, order, dst, bank, copy):
             w_turned = ps.tile([P, 2, P], F32, name=f"w_turned{b}", tag=bank)
             for u in order:
                 nc.tensor.transpose(w_turned[:, u, :], pairs[u].rearrange("q s e -> q (s e)").bitcast(F32), ident[:])
-            nc.scalar.copy(dst.bitcast(F32).rearrange("s (q u) -> s q u", u=2), w_turned[:].rearrange("s u q -> s q u"))
+            copy(dst.bitcast(F32).rearrange("s (q u) -> s q u", u=2), w_turned[:].rearrange("s u q -> s q u"))
 
         turn_values(0)
-        turn_weights(0, [w_pairs[0][:, u, :, :] for u in range(2)], (0, 1), vw0_bf[:, 1, :], "bank0_0")
-        turn_weights(1, [w_pairs[1][:, u, :, :] for u in range(2)], (0, 1), w1_bf[:], "bank0_1")
+        nc.vector.tensor_copy(picked[1][:, 0:SPLIT1], v_pool[1][:].indirect(slot_list[:, 0 : SPLIT1 // 16]))
+        nc.scalar.activation(picked[1][:, SPLIT1:N], v_pool[1][:].indirect(slot_list[:, SPLIT1 // 16 : N // 16]), ACT.Copy)
+        turn_weights(0, [w_pairs[0][:, u, :, :] for u in range(2)], (0, 1), vw0_bf[:, 1, :], "bank0_0", nc.scalar.copy)
+        turn_weights(1, [w_pairs[1][:, u, :, :] for u in range(2)], (0, 1), w1_bf[:], "bank0_1", nc.scalar.copy)
         inv_turned = ps.tile([P, QB, P], F32, name="inv_turned", tag="bank1_1")
         for b in range(QB):
             nc.tensor.transpose(inv_turned[:, b, :], inv_sum[:, b : b + 1].to_broadcast([P, P]), ident[:])
-        stage = staged.tile([P, HALF], BF16, name="stage", align_bytes=64, offset=4 * (2 * P - P // 2))
-        nc.vector.tensor_copy(stage[:], v_pool[1][:].indirect(slot_list[:, 0 : HALF // 16]))
-        nc.gpsimd.tensor_copy(picked[1][:, 0:HALF], stage[:])
-        nc.vector.tensor_copy(picked[1][:, HALF:N], v_pool[1][:].indirect(slot_list[:, HALF // 16 : N // 16]))
         turn_values(1)
-        codes = staged.tile([P, 3 * P], U32, name="codes", align_bytes=64, offset=0)
+        codes = reused.tile([P, 3 * P], U32, name="codes", align_bytes=64, offset=0)
         v_codes = [codes[:, 0:P], v1_codes[:]]
 
         nc.vector.quantize_mx(out=codes[:, 0 : 2 * P].bitcast(FP8X4), scales=scales[:, 0 : 2 * P],

@@ -206,8 +206,9 @@ def tile_attend_router_kernel(tc, xq, k_words, k_scales, vT, vs, offs, qoffs, ou
         codes = reused.tile([P, 3 * P], U32, name="codes", align_bytes=64, offset=0)
         v_codes = [codes[:, 0:P], v1_codes[:]]
 
-        nc.vector.quantize_mx(out=codes[:, 0 : 2 * P].bitcast(FP8X4), scales=scales[:, 0 : 2 * P],
-                              in_=vw0_bf[:].rearrange("s a n -> s (a n)"))
+        for a in range(2):
+            cols = slice(a * P, (a + 1) * P)
+            nc.vector.quantize_mx(out=codes[:, cols].bitcast(FP8X4), scales=scales[:, cols], in_=vw0_bf[:, a, :])
         product(0, 0, P, "bank0_0", nc.vector.tensor_copy)
         nc.vector.quantize_mx(out=codes[:, 2 * P : 3 * P].bitcast(FP8X4), scales=scales[:, 2 * P : 3 * P], in_=w1_bf[:])
         product(0, P, NQ, "bank0_1", nc.scalar.copy)

@@ -24,7 +24,8 @@ SCALE_STEP = P // (D // 32)
 VS_ROW = 4
 
 SPLIT = 320
-SPLIT1 = 384
+SPLIT1 = 416
+STAGED = 64
 
 FLOPS = 2 * NQ * N * (D + DV)
 BYTES = 4 * D * T + D * T + (D // 32) * T + 4 * DV * T + 4 * T + 2 * P * (N + NQ) // 16 + 4 * DV * T
@@ -36,6 +37,7 @@ def tile_attend_router_kernel(tc, xq, k_words, k_scales, vT, vs, offs, qoffs, ou
         sb = ctx.enter_context(tc.tile_pool(name="sb", bufs=1))
         reused = ctx.enter_context(tc.tile_pool(name="reused", bufs=1))
         reused0 = ctx.enter_context(tc.tile_pool(name="reused0", bufs=1))
+        staged = ctx.enter_context(tc.tile_pool(name="staged", bufs=1))
         after_q = ctx.enter_context(tc.tile_pool(name="after_q", bufs=1))
         after_sums = ctx.enter_context(tc.tile_pool(name="after_sums", bufs=1))
         ps = ctx.enter_context(tc.psum_pool(name="ps", bufs=1))
@@ -195,7 +197,10 @@ def tile_attend_router_kernel(tc, xq, k_words, k_scales, vT, vs, offs, qoffs, ou
             copy(dst.bitcast(F32).rearrange("s (q u) -> s q u", u=2), w_turned[:].rearrange("s u q -> s q u"))
 
         turn_values(0)
-        nc.vector.tensor_copy(picked[1][:, 0:SPLIT1], v_pool[1][:].indirect(slot_list[:, 0 : SPLIT1 // 16]))
+        stage = staged.tile([P, STAGED], BF16, name="stage", align_bytes=64, offset=0)
+        nc.vector.tensor_copy(stage[:], v_pool[1][:].indirect(slot_list[:, 0 : STAGED // 16]))
+        nc.gpsimd.tensor_copy(picked[1][:, 0:STAGED], stage[:])
+        nc.vector.tensor_copy(picked[1][:, STAGED:SPLIT1], v_pool[1][:].indirect(slot_list[:, STAGED // 16 : SPLIT1 // 16]))
         nc.scalar.activation(picked[1][:, SPLIT1:N], v_pool[1][:].indirect(slot_list[:, SPLIT1 // 16 : N // 16]), ACT.Copy)
         turn_weights(0, [w_pairs[0][:, u, :, :] for u in range(2)], (0, 1), vw0_bf[:, 1, :], "bank0_0", nc.scalar.copy)
         turn_weights(1, [w_pairs[1][:, u, :, :] for u in range(2)], (0, 1), w1_bf[:], "bank0_1", nc.scalar.copy)
@@ -203,7 +208,7 @@ def tile_attend_router_kernel(tc, xq, k_words, k_scales, vT, vs, offs, qoffs, ou
         for b in range(QB):
             nc.tensor.transpose(inv_turned[:, b, :], inv_sum[:, b : b + 1].to_broadcast([P, P]), ident[:])
         turn_values(1)
-        codes = reused.tile([P, 3 * P], U32, name="codes", align_bytes=64, offset=0)
+        codes = staged.tile([P, 3 * P], U32, name="codes", align_bytes=64, offset=0)
         v_codes = [codes[:, 0:P], v1_codes[:]]
 
         for a in range(2):

@@ -23,7 +23,7 @@ HALF = N // 2
 SCALE_STEP = P // (D // 32)
 VS_ROW = 4
 
-SPLIT = 320
+SPLIT = 288
 SPLIT1 = 416
 STAGED = 64
 

from contextlib import ExitStack

import concourse.mybir as mybir
from concourse.masks import make_identity

F32 = mybir.dt.float32
BF16 = mybir.dt.bfloat16
I32 = mybir.dt.int32
U32 = mybir.dt.uint32
U16 = mybir.dt.uint16
U8 = mybir.dt.uint8
FP8X4 = mybir.dt.float8_e4m3fn_x4
ACT = mybir.ActivationFunctionType
ALU = mybir.AluOpType
AX = mybir.AxisListType

P = 128
PACK = 4
T, D, DV, N, NQ = 2048, 512, 256, 512, 256
QB = NQ // P
EB = DV // P
HALF = N // 2
SCALE_STEP = P // (D // 32)
VS_ROW = 4

SPLIT = 288
SPLIT1 = 416
STAGED = 64

FLOPS = 2 * NQ * N * (D + DV)
BYTES = 4 * D * T + D * T + (D // 32) * T + 4 * DV * T + 4 * T + 2 * P * (N + NQ) // 16 + 4 * DV * T


def tile_attend_router_kernel(tc, xq, k_words, k_scales, vT, vs, offs, qoffs, out):
    nc = tc.nc
    with ExitStack() as ctx:
        sb = ctx.enter_context(tc.tile_pool(name="sb", bufs=1))
        reused = ctx.enter_context(tc.tile_pool(name="reused", bufs=1))
        reused0 = ctx.enter_context(tc.tile_pool(name="reused0", bufs=1))
        staged = ctx.enter_context(tc.tile_pool(name="staged", bufs=1))
        after_q = ctx.enter_context(tc.tile_pool(name="after_q", bufs=1))
        after_sums = ctx.enter_context(tc.tile_pool(name="after_sums", bufs=1))
        ps = ctx.enter_context(tc.psum_pool(name="ps", bufs=1))

        slot_list = sb.tile([P, N // 16], U16, name="slot_list")
        query_list = sb.tile([P, NQ // 16], U16, name="query_list")
        xq_pool = [reused0.tile([P, T], F32, name="xq_pool0", align_bytes=64, offset=0),
                   reused.tile([P, T], F32, name="xq_pool1", align_bytes=64, offset=0),
                   sb.tile([P, T], F32, name="xq_pool2"), sb.tile([P, T], F32, name="xq_pool3")]
        ks_pool = sb.tile([P, T], U8, name="ks_pool", tag="scales_then_words")
        vs_pool = sb.tile([P, T], F32, name="vs_pool")
        result = [sb.tile([P, T], F32, name=f"result{h}") for h in range(EB)]

        nc.gpsimd.memset(ks_pool[:].bitcast(I32), 0)
        nc.vector.memset(vs_pool[:], 0.0)

        xq_planes = xq.rearrange("(s t) n -> s t n", t=PACK)
        nc.sync.dma_start(xq_pool[0][:], xq_planes[:, 0, :])
        nc.sync.dma_start(slot_list[:], offs)
        nc.sync.dma_start(ks_pool[0:P:SCALE_STEP, :].bitcast(I32), k_scales[0].bitcast(I32))
        nc.sync.dma_start(query_list[:], qoffs)
        nc.sync.dma_start(xq_pool[1][:], xq_planes[:, 1, :])
        nc.sync.dma_start(vs_pool[VS_ROW : VS_ROW + 1, :], vs[0:1, :])
        nc.sync.dma_start(xq_pool[2][:], xq_planes[:, 2, :])
        nc.sync.dma_start(xq_pool[3][:], xq_planes[:, 3, :])

        ident = sb.tile([P, P], F32, name="ident")
        make_identity(nc, ident[:])
        for h in range(EB):
            nc.gpsimd.memset(result[h][:], 0.0)

        q_bf = after_q.tile([P, NQ, PACK], BF16, name="q_bf", align_bytes=64, offset=0)

        def gather_queries(t):
            nc.vector.tensor_copy(q_bf[:, :, t], xq_pool[t][:].indirect(query_list[:]))

        k_codes = sb.tile([P, N], U32, name="k_codes", align_bytes=64)
        k_bytes = sb.tile([P, N], U8, name="k_bytes", align_bytes=64)
        vs_row = sb.tile([P, N], F32, name="vs_row")
        ks_picked = sb.tile([P, N], U8, name="ks_picked")
        nc.vector.tensor_copy(ks_picked[:], ks_pool[:].indirect(slot_list[:]))
        nc.vector.tensor_copy(k_bytes[:].bitcast(I32), ks_picked[:].bitcast(I32))
        for r in range(1, 4):
            nc.sync.dma_start(k_bytes[r:P:32, :].bitcast(I32), ks_picked[r * SCALE_STEP : P : 32, :].bitcast(I32))

        kw_pool = sb.tile([P, T], I32, name="kw_pool", tag="scales_then_words")
        nc.sync.dma_start(kw_pool[:], k_words[0].rearrange("s n t -> s (n t)").bitcast(I32))
        gather_queries(0)
        v_pool = [reused0.tile([P, T], F32, name="v_pool0", align_bytes=64, offset=0)]
        nc.sync.dma_start(v_pool[0][:], vT[0:P, :])
        gather_queries(1)
        v_pool.append(reused.tile([P, T], F32, name="v_pool1", align_bytes=64, offset=0))
        nc.sync.dma_start(v_pool[1][:], vT[P : 2 * P, :])

        nc.vector.tensor_copy(vs_row[:].rearrange("q (u s e) -> q s u e", u=2, e=2), vs_pool[:].indirect(slot_list[:]))
        vs_turned = ps.tile([P, PACK, P], F32, name="vs_turned", tag="rows")
        for a in range(PACK):
            nc.tensor.transpose(vs_turned[:, a, :], vs_row[:, a * P : (a + 1) * P], ident[:])
        vs_col = sb.tile([P, PACK], F32, name="vs_col")
        nc.vector.tensor_copy(vs_col[:], vs_turned[:, :, VS_ROW])
        vs_wide = ps.tile([P, PACK, P], F32, name="vs_wide", tag="rows")
        for a in range(PACK):
            nc.tensor.transpose(vs_wide[:, a, :], vs_col[:, a : a + 1].to_broadcast([P, P]), ident[:])
        vs_pairs = vs_wide[:].rearrange("q (u h) (s e) -> q u (h s) e", u=2, e=2)

        gather_queries(2)
        gather_queries(3)

        q_codes = sb.tile([P, NQ], U32, name="q_codes", align_bytes=64)
        q_bytes = sb.tile([P, NQ], U8, name="q_bytes", align_bytes=64)
        q_flat = q_bf[:].rearrange("s q t -> s (q t)")
        for b in range(QB):
            cols = slice(b * P, (b + 1) * P)
            nc.vector.quantize_mx(out=q_codes[:, cols].bitcast(FP8X4), scales=q_bytes[:, cols],
                                  in_=q_flat[:, b * P * PACK : (b + 1) * P * PACK])

        vs_late = after_q.tile([P, 2, P // 2, 2], F32, name="vs_late", align_bytes=64, offset=0)
        nc.vector.tensor_copy(vs_late[:], vs_pairs[:, :, P // 2 : P, :])

        scores = [[ps.tile([P, HALF], F32, name=f"score{b}_{j}", tag=f"bank{b}_{j}") for j in range(2)]
                  for b in range(QB)]
        for j in range(2):
            slots = slice(j * HALF, (j + 1) * HALF)
            nc.vector.tensor_copy(k_codes[:, slots],
                                  kw_pool[:].bitcast(U32).indirect(slot_list[:, j * HALF // 16 : (j + 1) * HALF // 16]))
            for b in range(QB):
                cols = slice(b * P, (b + 1) * P)
                nc.tensor.matmul_mx(out=scores[b][j][:], lhsT=q_codes[:, cols].bitcast(FP8X4), lhsT_scale=q_bytes[:, cols],
                                    rhs=k_codes[:, slots].bitcast(FP8X4), rhs_scale=k_bytes[:, slots], start=True, stop=True)

        halves = [slice(0, P // 2), slice(P // 2, P)]
        by_pairs = [[scores[b][j][:].rearrange("q (s u e) -> q u s e", u=2, e=2) for j in range(2)] for b in range(QB)]
        neg_max = [[sb.tile([P, 1], F32, name=f"neg_max{b}_{j}") for j in range(2)] for b in range(QB)]
        neg_score = [sb.tile([P, 2, P // 2, 2], F32, name=f"neg_score{b}") for b in range(QB)]
        p = [[sb.tile([P, 2, P // 2, 2], F32, name=f"p{b}_{j}") for j in range(2)] for b in range(QB)]
        sum_parts = [sb.tile([P, 2], F32, name="sum_parts0"),
                     after_sums.tile([P, 2], F32, name="sum_parts1", align_bytes=64, offset=0)]
        nc.vector.tensor_reduce(neg_max[0][0][:], scores[0][0][:], AX.X, ALU.max, negate=True)
        nc.scalar.activation(p[0][0][:], by_pairs[0][0], ACT.Exp, bias=neg_max[0][0][:], accum_out=sum_parts[0][:, 0:1])
        nc.vector.tensor_reduce(neg_max[1][0][:], scores[1][0][:], AX.X, ALU.max, negate=True)
        for b in range(QB):
            nc.vector.tensor_scalar(neg_score[b][:], by_pairs[b][1], -1.0, neg_max[b][0][:], ALU.mult, ALU.min,
                                    accum_out=neg_max[b][1][:])

        picked = [sb.tile([P, N], BF16, name=f"v_picked{h}") for h in range(EB)]
        nc.scalar.activation(picked[0][:, SPLIT:N], v_pool[0][:].indirect(slot_list[:, SPLIT // 16 : N // 16]), ACT.Copy)
        nc.vector.tensor_copy(picked[0][:, 0:SPLIT], v_pool[0][:].indirect(slot_list[:, 0 : SPLIT // 16]))

        to_row_max = sb.tile([P, 1], F32, name="to_row_max")
        row_sum = sb.tile([P, QB], F32, name="row_sum")
        w_pairs = [sb.tile([P, 2, P, 2], BF16, name=f"w_pairs{b}") for b in range(QB)]
        nc.scalar.activation(to_row_max[:], neg_max[0][0][:], ACT.Exp, scale=-1.0, bias=neg_max[0][1][:])
        nc.scalar.activation(p[0][1][:], neg_score[0][:], ACT.Exp, scale=-1.0, bias=neg_max[0][1][:], accum_out=sum_parts[0][:, 1:2])
        nc.scalar.activation(p[1][0][:], by_pairs[1][0], ACT.Exp, bias=neg_max[1][1][:], accum_out=sum_parts[1][:, 0:1])
        nc.scalar.activation(p[1][1][:], neg_score[1][:], ACT.Exp, scale=-1.0, bias=neg_max[1][1][:], accum_out=sum_parts[1][:, 1:2])
        nc.scalar.activation(row_sum[:, 0:1], sum_parts[0][:, 0:1], ACT.Identity, scale=to_row_max[:], bias=sum_parts[0][:, 1:2])
        nc.scalar.activation(row_sum[:, 1:2], sum_parts[1][:, 0:1], ACT.Identity, bias=sum_parts[1][:, 1:2])
        flat = "q u s e -> q u (s e)"
        nc.vector.scalar_tensor_tensor(w_pairs[0][:, :, halves[0], :].rearrange(flat), p[0][0][:].rearrange(flat), to_row_max[:],
                                       vs_pairs[:, :, halves[0], :].rearrange(flat), ALU.mult, ALU.mult)
        nc.gpsimd.tensor_tensor(w_pairs[0][:, :, halves[1], :], p[0][1][:], vs_late[:], ALU.mult)
        for j in range(2):
            nc.vector.tensor_tensor(w_pairs[1][:, :, halves[j], :], p[1][j][:], vs_pairs[:, :, halves[j], :], ALU.mult)
        inv_sum = sb.tile([P, QB], F32, name="inv_sum")
        nc.vector.reciprocal(inv_sum[:], row_sum[:])

        vw0_bf = after_sums.tile([P, 2, N], BF16, name="vw0_bf", align_bytes=64, offset=0)
        v1_bf = sb.tile([P, N], BF16, name="v1_bf", align_bytes=64)
        w1_bf = sb.tile([P, N], BF16, name="w1_bf", align_bytes=64)
        scales = sb.tile([P, 3 * P], U8, name="scales", align_bytes=64)
        v1_codes = sb.tile([P, P], U32, name="v1_codes", align_bytes=64)
        v1_scales = sb.tile([P, P], U8, name="v1_scales", align_bytes=64)
        v_bf = [vw0_bf[:, 0, :], v1_bf[:]]
        v_scales = [scales[:, 0:P], v1_scales[:]]

        def turn_values(h):
            pairs = picked[h][:].bitcast(F32)
            v_turned = ps.tile([P, 2, P], F32, name=f"v_turned{h}", tag="v_turned")
            for u in range(2):
                nc.tensor.transpose(v_turned[:, u, :], pairs[:, u : N // 2 : 2], ident[:])
            nc.scalar.copy(v_bf[h].bitcast(F32).rearrange("s (f u) -> s f u", u=2), v_turned[:].rearrange("s u f -> s f u"))

        inv_wide = sb.tile([P, NQ], F32, name="inv_wide")
        y_sb = [sb.tile([P, NQ], F32, name=f"y_sb{h}") for h in range(EB)]

        def product(h, first, last, bank, copy):
            cols = slice(P + first, P + last)
            y = ps.tile([P, last - first], F32, name=f"y_{bank}", tag=bank)
            nc.tensor.matmul_mx(out=y[:], lhsT=v_codes[h].bitcast(FP8X4), lhsT_scale=v_scales[h],
                                rhs=codes[:, cols].bitcast(FP8X4), rhs_scale=scales[:, cols], start=True, stop=True)
            copy(y_sb[h][:, first:last], y[:])

        def turn_weights(b, pairs, order, dst, bank, copy):
            w_turned = ps.tile([P, 2, P], F32, name=f"w_turned{b}", tag=bank)
            for u in order:
                nc.tensor.transpose(w_turned[:, u, :], pairs[u].rearrange("q s e -> q (s e)").bitcast(F32), ident[:])
            copy(dst.bitcast(F32).rearrange("s (q u) -> s q u", u=2), w_turned[:].rearrange("s u q -> s q u"))

        turn_values(0)
        stage = staged.tile([P, STAGED], BF16, name="stage", align_bytes=64, offset=0)
        nc.vector.tensor_copy(stage[:], v_pool[1][:].indirect(slot_list[:, 0 : STAGED // 16]))
        nc.gpsimd.tensor_copy(picked[1][:, 0:STAGED], stage[:])
        nc.vector.tensor_copy(picked[1][:, STAGED:SPLIT1], v_pool[1][:].indirect(slot_list[:, STAGED // 16 : SPLIT1 // 16]))
        nc.scalar.activation(picked[1][:, SPLIT1:N], v_pool[1][:].indirect(slot_list[:, SPLIT1 // 16 : N // 16]), ACT.Copy)
        turn_weights(0, [w_pairs[0][:, u, :, :] for u in range(2)], (0, 1), vw0_bf[:, 1, :], "bank0_0", nc.scalar.copy)
        turn_weights(1, [w_pairs[1][:, u, :, :] for u in range(2)], (0, 1), w1_bf[:], "bank0_1", nc.scalar.copy)
        inv_turned = ps.tile([P, QB, P], F32, name="inv_turned", tag="bank1_1")
        for b in range(QB):
            nc.tensor.transpose(inv_turned[:, b, :], inv_sum[:, b : b + 1].to_broadcast([P, P]), ident[:])
        turn_values(1)
        codes = staged.tile([P, 3 * P], U32, name="codes", align_bytes=64, offset=0)
        v_codes = [codes[:, 0:P], v1_codes[:]]

        for a in range(2):
            cols = slice(a * P, (a + 1) * P)
            nc.vector.quantize_mx(out=codes[:, cols].bitcast(FP8X4), scales=scales[:, cols], in_=vw0_bf[:, a, :])
        product(0, 0, P, "bank0_0", nc.vector.tensor_copy)
        nc.vector.quantize_mx(out=codes[:, 2 * P : 3 * P].bitcast(FP8X4), scales=scales[:, 2 * P : 3 * P], in_=w1_bf[:])
        product(0, P, NQ, "bank0_1", nc.scalar.copy)
        nc.scalar.copy(inv_wide[:], inv_turned[:].rearrange("f b q -> f (b q)"))
        nc.vector.quantize_mx(out=v1_codes[:].bitcast(FP8X4), scales=v1_scales[:], in_=v1_bf[:])
        product(1, 0, NQ, "bank1_0", nc.scalar.copy)

        for h in range(EB):
            nc.vector.tensor_tensor(result[h][:].indirect(query_list[:]), y_sb[h][:], inv_wide[:], ALU.mult)
            nc.sync.dma_start(out[h * P : (h + 1) * P, :], result[h][:])
